import numpy as np
import ml_dtypes


def mxq(x, axis, fmt="e4m3"):
    dtype, down = {"e4m3": (ml_dtypes.float8_e4m3fn, 7), "e5m2": (ml_dtypes.float8_e5m2, 14)}[fmt]
    v = np.moveaxis(np.asarray(x, np.float32).astype(ml_dtypes.bfloat16).astype(np.float64), axis, -1)
    blocks = v.reshape(v.shape[:-1] + (-1, 32))
    amax = np.abs(blocks).max(-1, keepdims=True)
    byte = np.maximum(np.where(amax > 0, np.frexp(amax)[1] - 1 + 127, 0) - down, 1)
    scale = np.exp2(byte - 127.0)
    codes = (blocks / scale).astype(np.float32).astype(dtype).astype(np.float64)
    return np.moveaxis((codes * scale).reshape(v.shape), -1, axis)


WIDE = False


def mx_kscale(k):
    if not WIDE:
        return np.ones(k)
    levels = np.array([10, -10, 5, -5, 0])
    if k % 512:
        return np.exp2(np.random.permutation(np.resize(levels, k // 32))).repeat(32)
    a = np.empty((k // 512, 16))
    for p in range(k // 512):
        a[p, :8] = np.random.permutation(np.resize(levels, 8))
        for g in range(8):
            far = levels[np.abs(levels - a[p, g]) >= 10]
            a[p, g + 8] = far[np.random.randint(len(far))]
    return np.exp2(a.ravel()).repeat(32)


def f64(x):
    return np.asarray(x).astype(np.float64)


def striped(idx):
    return np.tile(idx.reshape(-1, 16).T, (8, 1)).astype(np.uint16)


def unstriped(offs):
    return offs[:16].T.reshape(-1).astype(np.int64)


E2M1 = np.array([0.0, 0.5, 1.0, 1.5, 2.0, 3.0, 4.0, 6.0, -0.0, -0.5, -1.0, -1.5, -2.0, -3.0, -4.0, -6.0])


def pack_weight(w, fmt):
    k, n = w.shape
    w = f64(np.asarray(w, np.float32).astype(ml_dtypes.bfloat16)).reshape(k // 32, 32, n)
    amax = np.abs(w).max(1)
    if fmt == "e4m3":
        byte = np.frexp(amax)[1] - 1 + 127 - 7
    else:
        mant, ex = np.frexp(amax / 6.0)
        byte = np.where(mant > 0.5, ex, ex - 1) + 127
    byte = np.clip(np.where(amax > 0, byte, 1), 1, 254)
    scaled = (w * np.exp2(127.0 - byte)[:, None, :]).reshape(k, n).astype(np.float32)
    by_word = np.ascontiguousarray(scaled.reshape(k // 512, 128, 4, n).transpose(0, 1, 3, 2))
    if fmt == "e4m3":
        words = by_word.astype(ml_dtypes.float8_e4m3fn).view(np.uint8)
    else:
        c = by_word.astype(ml_dtypes.float4_e2m1fn).view(np.uint8) & 0xF
        words = (c[..., 0::2] | (c[..., 1::2] << 4)).reshape(k // 512, 128, 2 * n)
    return np.ascontiguousarray(words), np.ascontiguousarray(byte.astype(np.uint8).reshape(k // 512, 16, n))


def unpack_weight(words, scales, fmt):
    g, _, n = scales.shape
    words = np.ascontiguousarray(words).reshape(g, 128, n, -1)
    if fmt == "e4m3":
        vals = words.view(ml_dtypes.float8_e4m3fn).astype(np.float64)
    else:
        nib = np.empty((g, 128, n, 4), np.uint8)
        nib[..., 0::2] = words & 0xF
        nib[..., 1::2] = words >> 4
        vals = E2M1[nib]
    vals = vals * np.repeat(np.exp2(scales.astype(np.float64) - 127.0), 8, axis=1)[..., None]
    return vals.transpose(0, 1, 3, 2).reshape(g * 512, n)


def gelu(v):
    return 0.5 * v * (1.0 + np.tanh(np.sqrt(2.0 / np.pi) * (v + 0.044715 * v**3)))


K, K2, H, N, T, TB, S, T2, P = 1024, 512, 1024, 512, 2048, 1024, 512, 2048, 1024

def setup_inputs():
    n = np.random.standard_normal
    s, s2, u = mx_kscale(K)[:, None], mx_kscale(K2)[:, None], mx_kscale(H)[:, None]
    d = {}
    d["tab_words"], d["tab_scales"] = pack_weight(n((K, T)) * s, "e4m3")
    d["tab2_words"], d["tab2_scales"] = pack_weight(n((K2, TB)) * s2, "e4m3")
    d["wa"] = (n((K, H)) / s / K ** 0.5).astype(np.float32)
    d["wb_words"], d["wb_scales"] = pack_weight(1.8 * n((K, H)) / s / K ** 0.5, "e2m1")
    d["wc"] = (1.3 * n((K2, H)) / s2 / K2 ** 0.5).astype(np.float32)
    d["bc"] = (0.9 * n(H)).astype(np.float32)
    d["page0"] = (1.5 * n((H, T2))).astype(np.float32)
    d["wg1"] = np.exp(0.3 * n((128, S))).astype(np.float32)
    d["wg2"] = np.exp(0.3 * n((128, S))).astype(np.float32)
    d["gain"] = (np.exp(0.3 * n(H)) * u[:, 0]).astype(np.float32)
    d["wo_words"], d["wo_scales"] = pack_weight(1.2 * n((H, N)) / u / H ** 0.5, "e4m3")
    perm = np.random.permutation(T2)
    d["offs"] = striped(np.random.permutation(T)[:S])
    d["offs2"] = striped(np.random.permutation(TB)[:S])
    d["offs3"] = striped(perm[:S])
    d["offs4"] = striped(perm[S:2 * S])
    d["offs5"] = striped(np.random.permutation(T2)[:P])
    return d

def reference(tab_words, tab_scales, tab2_words, tab2_scales, wa, wb_words, wb_scales, wc, bc, page0, wg1, wg2, gain, wo_words, wo_scales, offs, offs2, offs3, offs4, offs5):
    v = unpack_weight(tab_words, tab_scales, "e4m3")[:, unstriped(offs)]
    v2 = unpack_weight(tab2_words, tab2_scales, "e4m3")[:, unstriped(offs2)]
    a = mxq(f64(wa), 0, "e4m3").T @ v
    b = unpack_weight(wb_words, wb_scales, "e2m1").T @ v
    h1 = np.square(a - np.tanh(b))
    h2 = (mxq(f64(wc), 0, "e4m3").T @ v2) + f64(bc)[:, None]
    page = f64(page0).copy()
    page[:, unstriped(offs3)] = np.tile(f64(wg1), (H // 128, 1)) * h1
    page[:, unstriped(offs4)] = np.tile(f64(wg2), (H // 128, 1)) * h2
    x = np.log1p(np.abs(page[:, unstriped(offs5)])) * f64(gain)[:, None]
    return unpack_weight(wo_words, wo_scales, "e4m3").T @ mxq(x, 0, "e4m3")

@@ -1,0 +1,368 @@
+from contextlib import ExitStack
+
+import concourse.mybir as mybir
+from concourse.masks import make_identity
+
+K, K2, H, N, T, TB, S, T2, PICK = 1024, 512, 1024, 512, 2048, 1024, 512, 2048, 1024
+FLOPS = 2 * S * H * (2 * K + K2) + 2 * H * N * PICK
+
+F32 = mybir.dt.float32
+BF16 = mybir.dt.bfloat16
+I32 = mybir.dt.int32
+U32 = mybir.dt.uint32
+U16 = mybir.dt.uint16
+U8 = mybir.dt.uint8
+FP8X4 = mybir.dt.float8_e4m3fn_x4
+FP4X4 = mybir.dt.float4_e2m1fn_x4
+ACT = mybir.ActivationFunctionType
+MULT = mybir.AluOpType.mult
+
+P = 128
+PACK = 4
+KP = P * PACK
+SL = 256
+NS = PICK // SL
+
+
+def tile_list_reject_desk_scores_kernel(
+    tc, tab_words, tab_scales, tab2_words, tab2_scales, wa, wb_words, wb_scales, wc, bc, page0,
+    wg1, wg2, gain, wo_words, wo_scales, offs, offs2, offs3, offs4, offs5, out,
+):
+    nc = tc.nc
+    with ExitStack() as ctx:
+        keep = ctx.enter_context(tc.tile_pool(name="keep", bufs=1))
+        psum = ctx.enter_context(tc.psum_pool(name="psum", bufs=1))
+
+        def sb(name, shape, dtype):
+            return keep.tile(shape, dtype, name=name, align_bytes=64)
+
+        banks = [psum.tile([P, 512], F32, name="bank%d" % b) for b in range(8)]
+        list1 = sb("list1", [P, S // 16], U16)
+        list2 = sb("list2", [P, S // 16], U16)
+        list3 = sb("list3", [P, S // 16], U16)
+        list4 = sb("list4", [P, S // 16], U16)
+        list5 = sb("list5", [P, PICK // 16], U16)
+        tab_w = [sb("tab_w%d" % a, [P, T], U32) for a in range(2)]
+        tab_s = sb("tab_s", [P, 2 * T], U8)
+        tab2_w = sb("tab2_w", [P, TB], U32)
+        tab2_s = sb("tab2_s", [P, TB], U8)
+        v_w = [sb("v_w%d" % a, [P, S], U32) for a in range(2)]
+        v_s = [sb("v_s%d" % a, [P, S], U8) for a in range(2)]
+        v2_w = sb("v2_w", [P, S], U32)
+        v2_s = sb("v2_s", [P, S], U8)
+        wb_w = [sb("wb_w%d" % a, [P, 2 * H], U8) for a in range(2)]
+        wb_s = sb("wb_s", [P, 2 * H], U8)
+        wo_w = sb("wo_w", [P, 2 * N], U32)
+        wo_s = sb("wo_s", [P, 2 * N], U8)
+        bias = sb("bias", [P, 8], F32)
+        gains = sb("gains", [P, 8], F32)
+        ident = sb("ident", [P, P], F32)
+        wg1_d = [sb("wg1_d%d" % u, [P, 2 * S], F32) for u in range(2)]
+        wg2_d = [sb("wg2_d%d" % u, [P, 2 * S], F32) for u in range(2)]
+        pages = [sb("page%d" % i, [P, T2], F32) for i in range(4)]
+        raw = [sb("raw%d" % i, [P, PACK * KP], F32) for i in range(4)]
+        stage = [sb("stage%d" % i, [P, PACK * KP], BF16) for i in range(2)]
+        wc_w = [sb("wc_w%d" % h, [P, KP], U32) for h in range(2)]
+        wc_s = [sb("wc_s%d" % h, [P, KP], U8) for h in range(2)]
+        wa_w = [[sb("wa_w%d%d" % (h, a), [P, KP], U32) for a in range(2)] for h in range(2)]
+        wa_s = [[sb("wa_s%d%d" % (h, a), [P, KP], U8) for a in range(2)] for h in range(2)]
+        ntanh = [[sb("ntanh%d%d" % (h, jb), [P, KP], F32) for jb in range(4)] for h in range(2)]
+        a_t = [sb("a_t%d" % jb, [P, KP], F32) for jb in range(4)]
+        mix = sb("mix", [P, 2048], F32)
+        h1 = [sb("h1_%d" % t, [P, S], F32)[:] for t in range(2)] + [mix[:, 0:512], mix[:, 512:1024]]
+        h2 = [sb("h2_%d" % t, [P, S], F32) for t in range(4)]
+        picked = [sb("picked0", [P, PICK], F32)[:], mix[:, 1024:2048]]
+        picked.extend(sb("picked%d" % t, [P, PICK], F32)[:] for t in (2, 3))
+        picked.extend(raw[t][:, PICK:] for t in range(3))
+        warm = sb("warm", [P, 1], F32)
+        late = {}
+        x_w = [sb("x_w%d" % h, [P, PICK], U32) for h in range(2)]
+        x_bf = []
+        x_s = [sb("x_s%d" % h, [P, PICK], U8) for h in range(2)]
+
+        def load_scales(dst, src):
+            passes = src.shape[0]
+            for q in range(4):
+                nc.sync.dma_start(
+                    out=dst[32 * q : 32 * q + 4, :].bitcast(I32).rearrange("p (a c) -> p a c", a=passes),
+                    in_=src[:, 4 * q : 4 * q + 4, :].bitcast(I32).rearrange("a r c -> r a c"),
+                )
+
+        def load_words(dst, src):
+            nc.sync.dma_start(out=dst[:].bitcast(I32), in_=src.rearrange("p c i -> p (c i)").bitcast(I32))
+
+        def load_raw(dst, w, a, h):
+            nc.sync.dma_start(
+                out=dst[:].rearrange("p (i c) -> p i c", i=PACK),
+                in_=w[KP * a : KP * (a + 1), KP * h : KP * (h + 1)].rearrange("(p i) c -> p i c", i=PACK),
+            )
+
+        def load_gate(dst, wg, u):
+            rows = wg.rearrange("(m t) j -> m (t j)", t=PACK)[:, 2 * S * u : 2 * S * (u + 1)]
+            for q in range(4):
+                nc.sync.dma_start(out=dst[32 * q : 32 * (q + 1), :], in_=rows)
+
+        page_of = [0, 1, 2, 3, 1, 3, 1, 3]
+
+        def load_page(i):
+            h, t = divmod(i, PACK)
+            rows = page0[KP * h : KP * (h + 1), :].rearrange("(p t) c -> p t c", t=PACK)
+            nc.sync.dma_start(out=pages[page_of[i]][:], in_=rows[:, t, :])
+
+        def gather(dst, window, offsets):
+            nc.vector.tensor_copy(dst, window.indirect(offsets))
+
+        def quantize(words, scales, src):
+            nc.vector.quantize_mx(out=words.bitcast(FP8X4), scales=scales, in_=src)
+
+        def cast_wc(copy, dst, src):
+            copy(
+                dst.rearrange("p (t m i) -> p m i t", t=PACK, i=PACK),
+                src[:].rearrange("p (i m t) -> p m i t", i=PACK, t=PACK),
+            )
+
+        def cast_wa(copy, dst, src):
+            copy(
+                dst.rearrange("p (c e i) -> p c i e", e=4, i=PACK),
+                src[:].rearrange("p (i c e) -> p c i e", i=PACK, e=4),
+            )
+
+        def barcode(h, t):
+            bank = banks[4 + t % 2]
+            cols = slice(P * t, P * (t + 1))
+            nc.tensor.matmul_mx(
+                out=bank[:], lhsT=wc_w[h][:, cols].bitcast(FP8X4), lhsT_scale=wc_s[h][:, cols],
+                rhs=v2_w[:].bitcast(FP8X4), rhs_scale=v2_s[:], start=True, stop=True,
+            )
+            i = PACK * h + t
+            nc.scalar.activation(h2[t][:], bank[:], ACT.Identity, bias=bias[:, i : i + 1])
+
+        def line_product(jb, a, rhs, rhs_scale):
+            cols = slice(P * jb, P * (jb + 1))
+            nc.tensor.matmul_mx(
+                out=banks[jb][:], lhsT=v_w[a][:, cols].bitcast(FP8X4), lhsT_scale=v_s[a][:, cols],
+                rhs=rhs, rhs_scale=rhs_scale, start=(a == 0), stop=(a == 1),
+            )
+
+        def dealt_in(bank):
+            return bank[:].rearrange("p (m t) -> p t m", t=PACK)
+
+        def dealt_out(dst):
+            return dst[:].rearrange("p (t m) -> p t m", t=PACK)
+
+        def reading_b(h):
+            for a in range(2):
+                for jb in range(4):
+                    line_product(
+                        jb, a, wb_w[a][:, 2 * KP * h : 2 * KP * (h + 1)].bitcast(FP4X4),
+                        wb_s[:, H * a + KP * h : H * a + KP * (h + 1)],
+                    )
+            for jb in range(4):
+                nc.scalar.activation(dealt_out(ntanh[h][jb]), dealt_in(banks[jb]), ACT.Tanh, scale=-1.0)
+
+        def reading_a(h):
+            for a in range(2):
+                for jb in range(4):
+                    line_product(jb, a, wa_w[h][a][:].bitcast(FP8X4), wa_s[h][a][:])
+            for jb in range(4):
+                nc.scalar.copy(dealt_out(a_t[jb]), dealt_in(banks[jb]))
+
+        def mismatch(h, t):
+            bank = banks[6 + t % 2]
+            cols = slice(P * t, P * (t + 1))
+            for jb in range(4):
+                dst = bank[:, P * jb : P * (jb + 1)]
+                nc.tensor.matmul(dst, a_t[jb][:, cols], ident[:], start=True, stop=False, is_transpose=True)
+                nc.tensor.matmul(dst, ntanh[h][jb][:, cols], ident[:], start=False, stop=True, is_transpose=True)
+            nc.scalar.activation(h1[t], bank[:], ACT.Square)
+
+        def put_barcode(i):
+            t = i % PACK
+            gate = wg2_d[t // 2][:, S * (t % 2) : S * (t % 2 + 1)]
+            nc.vector.tensor_tensor(pages[page_of[i]][:].indirect(list4[:]), h2[t][:], gate, MULT)
+
+        def put_line(i):
+            t = i % PACK
+            gate = wg1_d[t // 2][:, S * (t % 2) : S * (t % 2 + 1)]
+            nc.vector.tensor_tensor(pages[page_of[i]][:].indirect(list3[:]), h1[t], gate, MULT)
+
+        def woven(h, t, cols):
+            return x_bf[h][:].rearrange("p (j t) -> p j t", t=PACK)[:, cols, t]
+
+        def fetch(i):
+            gather(picked[i], pages[page_of[i]][:], list5[:])
+
+        def compress(i):
+            h, t = divmod(i, PACK)
+            halves = [slice(S * u, S * (u + 1)) for u in range(2)]
+            for c in halves:
+                nc.scalar.activation(picked[i][:, c], picked[i][:, c], ACT.Abs)
+            for c in halves:
+                nc.scalar.activation(picked[i][:, c], picked[i][:, c], ACT.Ln, bias=1.0)
+            for c in halves:
+                dst = late["planes"][:, PICK * t : PICK * (t + 1)][:, c] if h == 0 else woven(1, t, c)
+                nc.scalar.activation(dst, picked[i][:, c], ACT.Copy, scale=gains[:, i : i + 1])
+
+        def weave():
+            nc.scalar.copy(
+                x_bf[0][:].rearrange("p (c e t) -> p c t e", e=4, t=PACK),
+                late["planes"][:].rearrange("p (t c e) -> p c t e", t=PACK, e=4),
+            )
+
+        def score(s, h):
+            cols = slice(SL * s, SL * (s + 1))
+            for n in range(4):
+                nc.tensor.matmul_mx(
+                    out=banks[2 * s + n // 2][:, SL * (n % 2) : SL * (n % 2 + 1)],
+                    lhsT=wo_w[:, N * h + P * n : N * h + P * (n + 1)].bitcast(FP8X4),
+                    lhsT_scale=wo_s[:, N * h + P * n : N * h + P * (n + 1)],
+                    rhs=x_w[h][:, cols].bitcast(FP8X4), rhs_scale=x_s[h][:, cols],
+                    start=(h == 0 and n % 2 == 0), stop=(h == 1 and n % 2 == 1),
+                )
+
+        for plane in (tab2_s, tab_s):
+            nc.gpsimd.memset(plane[:].bitcast(I32), 0)
+        for plane in (wb_s, wo_s):
+            nc.vector.memset(plane[:].bitcast(I32), 0)
+        nc.vector.memset(warm[:], 0.0)
+        nc.scalar.activation(warm[:], warm[:], ACT.Tanh)
+        make_identity(nc, ident[:])
+
+        def load_column(dst, vec):
+            nc.sync.dma_start(
+                out=dst[:].rearrange("p (h t) -> p h t", t=PACK), in_=vec.rearrange("(h p t) -> p h t", h=2, t=PACK)
+            )
+
+        def load_wb(h):
+            for a in range(2):
+                cols = slice(2 * KP * h, 2 * KP * (h + 1))
+                nc.sync.dma_start(out=wb_w[a][:, cols].bitcast(I32), in_=wb_words[a][:, cols].bitcast(I32))
+
+        load_words(tab2_w, tab2_words[0])
+        nc.sync.dma_start(list2[:], offs2)
+        load_scales(tab2_s, tab2_scales)
+        load_raw(raw[0], wc, 0, 0)
+        nc.sync.dma_start(list1[:], offs)
+        load_scales(tab_s, tab_scales)
+        load_page(0)
+        nc.sync.dma_start(list4[:], offs4)
+        load_gate(wg2_d[0], wg2, 0)
+        load_column(bias, bc)
+        load_words(tab_w[0], tab_words[0])
+        load_words(tab_w[1], tab_words[1])
+        load_scales(wb_s, wb_scales)
+        load_wb(0)
+        load_raw(raw[1], wa, 0, 0)
+        load_page(1)
+        load_raw(raw[2], wa, 1, 0)
+        load_gate(wg2_d[1], wg2, 1)
+        load_page(2)
+        nc.sync.dma_start(list3[:], offs3)
+        load_gate(wg1_d[0], wg1, 0)
+        load_page(3)
+        load_wb(1)
+        nc.sync.dma_start(list5[:], offs5)
+        load_column(gains, gain)
+        load_raw(raw[3], wc, 0, 1)
+
+        gather(v2_s[:], tab2_s[:], list2[:])
+        gather(v2_w[:], tab2_w[:], list2[:])
+        for u in range(2):
+            half = stage[0][:, 1024 * u : 1024 * (u + 1)]
+            nc.scalar.copy(
+                half.rearrange("p (t m i) -> p m i t", t=2, i=PACK),
+                raw[0][:].rearrange("p (i m t) -> p m i t", i=PACK, t=PACK)[:, :, :, 2 * u : 2 * u + 2],
+            )
+            quantize(wc_w[0][:, 256 * u : 256 * (u + 1)], wc_s[0][:, 256 * u : 256 * (u + 1)], half)
+        load_raw(raw[0], wa, 0, 1)
+        for t in range(PACK):
+            barcode(0, t)
+        put_barcode(0)
+        for a in range(2):
+            gather(v_s[a][:], tab_s[:, T * a : T * (a + 1)], list1[:])
+        gather(v_w[0][:], tab_w[0][:], list1[:])
+        gather(v_w[1][:], tab_w[1][:], list1[:])
+        reading_b(0)
+        for a in range(2):
+            cast_wa(nc.vector.tensor_copy, stage[1 - a][:], raw[1 + a])
+            quantize(wa_w[0][a][:], wa_s[0][a][:], stage[1 - a][:])
+        load_raw(raw[1], wa, 1, 1)
+        load_gate(wg1_d[1], wg1, 1)
+        load_scales(wo_s, wo_scales)
+        nc.sync.dma_start(
+            out=wo_w[:].bitcast(I32).rearrange("p (a c) -> p a c", a=2),
+            in_=wo_words.rearrange("a p c i -> p a (c i)").bitcast(I32),
+        )
+        reading_a(0)
+        for t in range(1, PACK):
+            put_barcode(t)
+        for t in range(2):
+            mismatch(0, t)
+            put_line(t)
+        reading_b(1)
+        cast_wc(nc.scalar.copy, stage[1][:], raw[3])
+        quantize(wc_w[1][:], wc_s[1][:], stage[1][:])
+        for a, region in enumerate((picked[0], mix[:, 256:1280])):
+            cast_wa(nc.scalar.copy, region.bitcast(BF16), raw[a])
+            quantize(wa_w[1][a][:], wa_s[1][a][:], region.bitcast(BF16))
+        for t in range(2, PACK):
+            mismatch(0, t)
+        fetch(0)
+        fetch(1)
+        load_page(4)
+        for t in range(2, PACK):
+            put_line(t)
+            fetch(t)
+        load_page(5)
+        for t in range(PACK):
+            barcode(1, t)
+        reading_a(1)
+        for t in range(PACK):
+            mismatch(1, t)
+        late["planes"] = keep.tile([P, PICK * PACK], BF16, name="planes", tag="page0", align_bytes=64)
+        for h in range(2):
+            x_bf.append(keep.tile([P, PICK * PACK], BF16, name="x_bf%d" % h, tag="tab_w%d" % h, align_bytes=64))
+        for t in range(PACK):
+            compress(t)
+        weave()
+        for i in range(4, 7):
+            put_barcode(i)
+            put_line(i)
+            fetch(i)
+            compress(i)
+            if i + 2 < 8:
+                load_page(i + 2)
+        quantize(x_w[0][:], x_s[0][:], x_bf[0][:])
+        put_barcode(7)
+        put_line(7)
+        for s in range(NS):
+            score(s, 0)
+        ring = x_bf[0][:].bitcast(F32)
+
+        def finish(s):
+            cols = slice(SL * s, SL * (s + 1))
+            last = ring[:, cols]
+            gather(last, pages[page_of[7]][:], list5[:, SL // 16 * s : SL // 16 * (s + 1)])
+            nc.scalar.activation(last, last, ACT.Abs)
+            nc.scalar.activation(last, last, ACT.Ln, bias=1.0)
+            nc.vector.tensor_scalar(woven(1, 3, cols), last, gains[:, 7:8], None, MULT)
+            quantize(x_w[1][:, cols], x_s[1][:, cols], x_bf[1][:, PACK * SL * s : PACK * SL * (s + 1)])
+            score(s, 1)
+
+        def store(s):
+            cols = slice(SL * s, SL * (s + 1))
+            for u in range(2):
+                staged = raw[s][:, 512 * u : 512 * (u + 1)]
+                if u == 0 and s >= NS - 2:
+                    nc.vector.tensor_copy(staged, banks[2 * s + u][:])
+                else:
+                    nc.scalar.copy(staged, banks[2 * s + u][:])
+                nc.sync.dma_start(
+                    out=out[2 * P * u : 2 * P * (u + 1), cols].rearrange("(n p) c -> p n c", p=P),
+                    in_=staged.rearrange("p (n c) -> p n c", n=2),
+                )
+
+        for s in range(NS):
+            finish(s)
+        for s in range(NS):
+            store(s)

@@ -43,22 +43,26 @@ def tile_list_reject_desk_scores_kernel(
         list4 = sb("list4", [P, S // 16], U16)
         list5 = sb("list5", [P, PICK // 16], U16)
         tab_w = [sb("tab_w%d" % a, [P, T], U32) for a in range(2)]
-        tab_s = sb("tab_s", [P, 2 * T], U8)
+        tab_s = sb("tab_s", [P, T], U8)
+        v_rows = sb("v_rows", [P, S], U8)
         tab2_w = sb("tab2_w", [P, TB], U32)
         tab2_s = sb("tab2_s", [P, TB], U8)
         v_w = [sb("v_w%d" % a, [P, S], U32) for a in range(2)]
         v_s = [sb("v_s%d" % a, [P, S], U8) for a in range(2)]
         v2_w = sb("v2_w", [P, S], U32)
         v2_s = sb("v2_s", [P, S], U8)
-        wb_w = [sb("wb_w%d" % a, [P, 2 * H], U8) for a in range(2)]
-        wb_s = sb("wb_s", [P, 2 * H], U8)
+        wb_w = [sb("wb_w0", [P, 4 * KP], U8)[:], sb("wb_w1", [P, 20 * H], U8)[:, : 4 * KP]]
+        wb_s = [sb("wb_s%d" % h, [P, 2 * KP], U8) for h in range(2)]
         wo_w = sb("wo_w", [P, 2 * N], U32)
         wo_s = sb("wo_s", [P, 2 * N], U8)
         bias = sb("bias", [P, 8], F32)
         gains = sb("gains", [P, 8], F32)
         ident = sb("ident", [P, P], F32)
-        wg1_d = [sb("wg1_d%d" % u, [P, 2 * S], F32) for u in range(2)]
-        wg2_d = [sb("wg2_d%d" % u, [P, 2 * S], F32) for u in range(2)]
+        wg1_n = sb("wg1_n", [P, S], F32)
+        wg2_n = sb("wg2_n", [P, S], F32)
+        turned = [sb("turned%d" % u, [P, S], F32) for u in range(2)]
+        wg1_d = [sb("wg1_d%d" % t, [P, S], F32) for t in range(PACK)]
+        wg2_d = [sb("wg2_d%d" % t, [P, S], F32) for t in range(PACK)]
         pages = [sb("page%d" % i, [P, T2], F32) for i in range(4)]
         raw = [sb("raw%d" % i, [P, PACK * KP], F32) for i in range(4)]
         stage = [sb("stage%d" % i, [P, PACK * KP], BF16) for i in range(2)]
@@ -68,21 +72,20 @@ def tile_list_reject_desk_scores_kernel(
         wa_s = [[sb("wa_s%d%d" % (h, a), [P, KP], U8) for a in range(2)] for h in range(2)]
         ntanh = [[sb("ntanh%d%d" % (h, jb), [P, KP], F32) for jb in range(4)] for h in range(2)]
         a_t = [sb("a_t%d" % jb, [P, KP], F32) for jb in range(4)]
-        mix = sb("mix", [P, 2048], F32)
-        h1 = [sb("h1_%d" % t, [P, S], F32)[:] for t in range(2)] + [mix[:, 0:512], mix[:, 512:1024]]
+        h1 = [sb("h1_%d" % t, [P, S], F32)[:] for t in range(2)]
         h2 = [sb("h2_%d" % t, [P, S], F32) for t in range(4)]
-        picked = [sb("picked0", [P, PICK], F32)[:], mix[:, 1024:2048]]
-        picked.extend(sb("picked%d" % t, [P, PICK], F32)[:] for t in (2, 3))
-        picked.extend(raw[t][:, PICK:] for t in range(3))
+        picked = {t: sb("picked%d" % t, [P, PICK], F32)[:] for t in (2, 3)}
+        for t in range(3):
+            picked[4 + t] = raw[t][:, PICK:]
         warm = sb("warm", [P, 1], F32)
         late = {}
         x_w = [sb("x_w%d" % h, [P, PICK], U32) for h in range(2)]
         x_bf = []
         x_s = [sb("x_s%d" % h, [P, PICK], U8) for h in range(2)]
 
-        def load_scales(dst, src):
+        def load_scales(dst, src, quadrants):
             passes = src.shape[0]
-            for q in range(4):
+            for q in quadrants:
                 nc.sync.dma_start(
                     out=dst[32 * q : 32 * q + 4, :].bitcast(I32).rearrange("p (a c) -> p a c", a=passes),
                     in_=src[:, 4 * q : 4 * q + 4, :].bitcast(I32).rearrange("a r c -> r a c"),
@@ -97,12 +100,29 @@ def tile_list_reject_desk_scores_kernel(
                 in_=w[KP * a : KP * (a + 1), KP * h : KP * (h + 1)].rearrange("(p i) c -> p i c", i=PACK),
             )
 
-        def load_gate(dst, wg, u):
-            rows = wg.rearrange("(m t) j -> m (t j)", t=PACK)[:, 2 * S * u : 2 * S * (u + 1)]
-            for q in range(4):
-                nc.sync.dma_start(out=dst[32 * q : 32 * (q + 1), :], in_=rows)
+        def turn_gate(natural):
+            for jb in range(4):
+                cols = slice(P * jb, P * (jb + 1))
+                nc.tensor.transpose(banks[6][:, cols], natural[:, cols], ident[:])
 
-        page_of = [0, 1, 2, 3, 1, 3, 1, 3]
+        def deal_gate(dst, t, bank):
+            rows = banks[6][:].rearrange("p (jb m t) -> p jb m t", jb=4, t=PACK)[:, :, :, t]
+            nc.scalar.copy(
+                turned[t % 2][:].rearrange("p (jb q m) -> p jb q m", jb=4, q=4),
+                rows.unsqueeze(2).to_broadcast([P, 4, 4, 32]),
+            )
+            for jb in range(4):
+                cols = slice(P * jb, P * (jb + 1))
+                nc.tensor.transpose(bank[:, cols], turned[t % 2][:, cols], ident[:])
+            nc.scalar.copy(dst[:], bank[:])
+
+        def move_scales(a, q):
+            first = 16 * a + 4 * q
+            nc.sync.dma_start(
+                out=v_s[a][32 * q : 32 * q + 4, :].bitcast(I32), in_=v_rows[first : first + 4, :].bitcast(I32)
+            )
+
+        page_of = [0, 1, 2, 3, 1, 2, 3, 1]
 
         def load_page(i):
             h, t = divmod(i, PACK)
@@ -115,20 +135,28 @@ def tile_list_reject_desk_scores_kernel(
         def quantize(words, scales, src):
             nc.vector.quantize_mx(out=words.bitcast(FP8X4), scales=scales, in_=src)
 
-        def cast_wc(copy, dst, src):
-            copy(
-                dst.rearrange("p (t m i) -> p m i t", t=PACK, i=PACK),
-                src[:].rearrange("p (i m t) -> p m i t", i=PACK, t=PACK),
-            )
+        def make_wc(h, staged, src, copy):
+            for u in range(2):
+                half = staged[:, 1024 * u : 1024 * (u + 1)]
+                copy(
+                    half.rearrange("p (t m i) -> p m i t", t=2, i=PACK),
+                    src[:].rearrange("p (i m t) -> p m i t", i=PACK, t=PACK)[:, :, :, 2 * u : 2 * u + 2],
+                )
+            for u in range(2):
+                half = staged[:, 1024 * u : 1024 * (u + 1)]
+                quantize(wc_w[h][:, 256 * u : 256 * (u + 1)], wc_s[h][:, 256 * u : 256 * (u + 1)], half)
 
-        def cast_wa(copy, dst, src):
-            copy(
-                dst.rearrange("p (c e i) -> p c i e", e=4, i=PACK),
-                src[:].rearrange("p (i c e) -> p c i e", i=PACK, e=4),
-            )
+        def make_wa(h, a, staged, src, copy):
+            for u in range(2):
+                c = slice(64 * u, 64 * (u + 1))
+                copy(
+                    staged.rearrange("p (c e i) -> p c i e", e=4, i=PACK)[:, c],
+                    src[:].rearrange("p (i c e) -> p c i e", i=PACK, e=4)[:, c],
+                )
+            quantize(wa_w[h][a][:], wa_s[h][a][:], staged)
 
         def barcode(h, t):
-            bank = banks[4 + t % 2]
+            bank = banks[(4, 2)[h] + t % 2]
             cols = slice(P * t, P * (t + 1))
             nc.tensor.matmul_mx(
                 out=bank[:], lhsT=wc_w[h][:, cols].bitcast(FP8X4), lhsT_scale=wc_s[h][:, cols],
@@ -137,10 +165,10 @@ def tile_list_reject_desk_scores_kernel(
             i = PACK * h + t
             nc.scalar.activation(h2[t][:], bank[:], ACT.Identity, bias=bias[:, i : i + 1])
 
-        def line_product(jb, a, rhs, rhs_scale):
+        def line_product(bank, jb, a, rhs, rhs_scale):
             cols = slice(P * jb, P * (jb + 1))
             nc.tensor.matmul_mx(
-                out=banks[jb][:], lhsT=v_w[a][:, cols].bitcast(FP8X4), lhsT_scale=v_s[a][:, cols],
+                out=bank[:], lhsT=v_w[a][:, cols].bitcast(FP8X4), lhsT_scale=v_s[a][:, cols],
                 rhs=rhs, rhs_scale=rhs_scale, start=(a == 0), stop=(a == 1),
             )
 
@@ -150,25 +178,26 @@ def tile_list_reject_desk_scores_kernel(
         def dealt_out(dst):
             return dst[:].rearrange("p (t m) -> p t m", t=PACK)
 
-        def reading_b(h):
-            for a in range(2):
-                for jb in range(4):
-                    line_product(
-                        jb, a, wb_w[a][:, 2 * KP * h : 2 * KP * (h + 1)].bitcast(FP4X4),
-                        wb_s[:, H * a + KP * h : H * a + KP * (h + 1)],
-                    )
-            for jb in range(4):
-                nc.scalar.activation(dealt_out(ntanh[h][jb]), dealt_in(banks[jb]), ACT.Tanh, scale=-1.0)
+        def product_b(bank, h, jb, a):
+            line_product(
+                bank, jb, a, wb_w[h][:, 2 * KP * a : 2 * KP * (a + 1)].bitcast(FP4X4),
+                wb_s[h][:, KP * a : KP * (a + 1)],
+            )
+
+        def tanh_b(bank, h, jb):
+            nc.scalar.activation(dealt_out(ntanh[h][jb]), dealt_in(bank), ACT.Tanh, scale=-1.0)
 
         def reading_a(h):
             for a in range(2):
                 for jb in range(4):
-                    line_product(jb, a, wa_w[h][a][:].bitcast(FP8X4), wa_s[h][a][:])
-            for jb in range(4):
-                nc.scalar.copy(dealt_out(a_t[jb]), dealt_in(banks[jb]))
+                    line_product(banks[4 + jb], jb, a, wa_w[h][a][:].bitcast(FP8X4), wa_s[h][a][:])
+            for u in range(2):
+                for jb in range(4):
+                    pair = slice(2 * u, 2 * u + 2)
+                    nc.scalar.copy(dealt_out(a_t[jb])[:, pair, :], dealt_in(banks[4 + jb])[:, pair, :])
 
         def mismatch(h, t):
-            bank = banks[6 + t % 2]
+            bank = banks[t % 2]
             cols = slice(P * t, P * (t + 1))
             for jb in range(4):
                 dst = bank[:, P * jb : P * (jb + 1)]
@@ -178,12 +207,12 @@ def tile_list_reject_desk_scores_kernel(
 
         def put_barcode(i):
             t = i % PACK
-            gate = wg2_d[t // 2][:, S * (t % 2) : S * (t % 2 + 1)]
+            gate = wg2_d[t][:]
             nc.vector.tensor_tensor(pages[page_of[i]][:].indirect(list4[:]), h2[t][:], gate, MULT)
 
         def put_line(i):
             t = i % PACK
-            gate = wg1_d[t // 2][:, S * (t % 2) : S * (t % 2 + 1)]
+            gate = wg1_d[t][:]
             nc.vector.tensor_tensor(pages[page_of[i]][:].indirect(list3[:]), h1[t], gate, MULT)
 
         def woven(h, t, cols):
@@ -193,21 +222,23 @@ def tile_list_reject_desk_scores_kernel(
             gather(picked[i], pages[page_of[i]][:], list5[:])
 
         def compress(i):
-            h, t = divmod(i, PACK)
+            t = i % PACK
             halves = [slice(S * u, S * (u + 1)) for u in range(2)]
             for c in halves:
                 nc.scalar.activation(picked[i][:, c], picked[i][:, c], ACT.Abs)
             for c in halves:
                 nc.scalar.activation(picked[i][:, c], picked[i][:, c], ACT.Ln, bias=1.0)
             for c in halves:
-                dst = late["planes"][:, PICK * t : PICK * (t + 1)][:, c] if h == 0 else woven(1, t, c)
+                dst = late["planes"][:, PICK * t : PICK * (t + 1)][:, c]
                 nc.scalar.activation(dst, picked[i][:, c], ACT.Copy, scale=gains[:, i : i + 1])
 
-        def weave():
-            nc.scalar.copy(
-                x_bf[0][:].rearrange("p (c e t) -> p c t e", e=4, t=PACK),
-                late["planes"][:].rearrange("p (t c e) -> p c t e", t=PACK, e=4),
-            )
+        def weave(h, count):
+            for u in range(2):
+                c = slice(P * u, P * (u + 1))
+                nc.scalar.copy(
+                    x_bf[h][:].rearrange("p (c e t) -> p c t e", e=4, t=PACK)[:, c, :count, :],
+                    late["planes"][:].rearrange("p (t c e) -> p c t e", t=PACK, e=4)[:, c, :count, :],
+                )
 
         def score(s, h):
             cols = slice(SL * s, SL * (s + 1))
@@ -220,9 +251,9 @@ def tile_list_reject_desk_scores_kernel(
                     start=(h == 0 and n % 2 == 0), stop=(h == 1 and n % 2 == 1),
                 )
 
-        for plane in (tab2_s, tab_s):
-            nc.gpsimd.memset(plane[:].bitcast(I32), 0)
-        for plane in (wb_s, wo_s):
+        for unused in (slice(32, 64), slice(64, P)):
+            nc.vector.memset(tab_s[unused, :].bitcast(I32), 0)
+        for plane in (tab2_s, wb_s[0], v_s[0], v_s[1], wb_s[1], wo_s):
             nc.vector.memset(plane[:].bitcast(I32), 0)
         nc.vector.memset(warm[:], 0.0)
         nc.scalar.activation(warm[:], warm[:], ACT.Tanh)
@@ -234,61 +265,73 @@ def tile_list_reject_desk_scores_kernel(
             )
 
         def load_wb(h):
-            for a in range(2):
-                cols = slice(2 * KP * h, 2 * KP * (h + 1))
-                nc.sync.dma_start(out=wb_w[a][:, cols].bitcast(I32), in_=wb_words[a][:, cols].bitcast(I32))
+            nc.sync.dma_start(
+                out=wb_w[h].bitcast(I32).rearrange("p (a c) -> p a c", a=2),
+                in_=wb_words[:, :, 2 * KP * h : 2 * KP * (h + 1)].bitcast(I32).rearrange("a p c -> p a c"),
+            )
 
-        load_words(tab2_w, tab2_words[0])
-        nc.sync.dma_start(list2[:], offs2)
-        load_scales(tab2_s, tab2_scales)
-        load_raw(raw[0], wc, 0, 0)
+        nc.sync.dma_start(out=wg2_n[:], in_=wg2)
         nc.sync.dma_start(list1[:], offs)
-        load_scales(tab_s, tab_scales)
-        load_page(0)
+        nc.sync.dma_start(
+            out=tab_s[0:32, :].bitcast(I32), in_=tab_scales.rearrange("a r c -> (a r) c").bitcast(I32)
+        )
+        nc.sync.dma_start(list2[:], offs2)
+        load_words(tab2_w, tab2_words[0])
+        load_raw(raw[0], wc, 0, 0)
         nc.sync.dma_start(list4[:], offs4)
-        load_gate(wg2_d[0], wg2, 0)
         load_column(bias, bc)
+        load_scales(tab2_s, tab2_scales, (0, 2, 1, 3))
+        load_page(0)
+        gather(v_rows[:], tab_s[:], list1[:])
+        for q in range(4):
+            move_scales(0, q)
         load_words(tab_w[0], tab_words[0])
+        nc.sync.dma_start(out=wg1_n[:], in_=wg1)
+        for q in range(2):
+            move_scales(1, q)
         load_words(tab_w[1], tab_words[1])
-        load_scales(wb_s, wb_scales)
-        load_wb(0)
+        for q in range(2, 4):
+            move_scales(1, q)
+        load_scales(wb_s[0], wb_scales[:, :, :KP], (0, 2))
         load_raw(raw[1], wa, 0, 0)
+        load_scales(wb_s[0], wb_scales[:, :, :KP], (1, 3))
+        load_wb(0)
         load_page(1)
         load_raw(raw[2], wa, 1, 0)
-        load_gate(wg2_d[1], wg2, 1)
         load_page(2)
         nc.sync.dma_start(list3[:], offs3)
-        load_gate(wg1_d[0], wg1, 0)
         load_page(3)
         load_wb(1)
+        load_scales(wb_s[1], wb_scales[:, :, KP:], (0, 2, 1, 3))
         nc.sync.dma_start(list5[:], offs5)
         load_column(gains, gain)
         load_raw(raw[3], wc, 0, 1)
-
-        gather(v2_s[:], tab2_s[:], list2[:])
         gather(v2_w[:], tab2_w[:], list2[:])
-        for u in range(2):
-            half = stage[0][:, 1024 * u : 1024 * (u + 1)]
-            nc.scalar.copy(
-                half.rearrange("p (t m i) -> p m i t", t=2, i=PACK),
-                raw[0][:].rearrange("p (i m t) -> p m i t", i=PACK, t=PACK)[:, :, :, 2 * u : 2 * u + 2],
-            )
-            quantize(wc_w[0][:, 256 * u : 256 * (u + 1)], wc_s[0][:, 256 * u : 256 * (u + 1)], half)
+
+        turn_gate(wg2_n)
+        deal_gate(wg2_d[0], 0, banks[0])
+        make_wc(0, stage[0][:], raw[0], nc.vector.tensor_copy)
+        gather(v2_s[:], tab2_s[:], list2[:])
         load_raw(raw[0], wa, 0, 1)
-        for t in range(PACK):
-            barcode(0, t)
+        barcode(0, 0)
         put_barcode(0)
-        for a in range(2):
-            gather(v_s[a][:], tab_s[:, T * a : T * (a + 1)], list1[:])
+        for t in range(1, PACK):
+            deal_gate(wg2_d[t], t, banks[t])
+            barcode(0, t)
+        turn_gate(wg1_n)
         gather(v_w[0][:], tab_w[0][:], list1[:])
         gather(v_w[1][:], tab_w[1][:], list1[:])
-        reading_b(0)
+        for t in range(PACK):
+            deal_gate(wg1_d[t], t, banks[4 + t % 2])
         for a in range(2):
-            cast_wa(nc.vector.tensor_copy, stage[1 - a][:], raw[1 + a])
-            quantize(wa_w[0][a][:], wa_s[0][a][:], stage[1 - a][:])
+            for jb in range(4):
+                product_b(banks[jb], 0, jb, a)
+        for jb in range(4):
+            tanh_b(banks[jb], 0, jb)
+        make_wa(0, 0, stage[1][:], raw[1], nc.vector.tensor_copy)
+        make_wa(0, 1, stage[0][:], raw[2], nc.vector.tensor_copy)
         load_raw(raw[1], wa, 1, 1)
-        load_gate(wg1_d[1], wg1, 1)
-        load_scales(wo_s, wo_scales)
+        load_scales(wo_s, wo_scales, range(4))
         nc.sync.dma_start(
             out=wo_w[:].bitcast(I32).rearrange("p (a c) -> p a c", a=2),
             in_=wo_words.rearrange("a p c i -> p a (c i)").bitcast(I32),
@@ -299,39 +342,46 @@ def tile_list_reject_desk_scores_kernel(
         for t in range(2):
             mismatch(0, t)
             put_line(t)
-        reading_b(1)
-        cast_wc(nc.scalar.copy, stage[1][:], raw[3])
-        quantize(wc_w[1][:], wc_s[1][:], stage[1][:])
-        for a, region in enumerate((picked[0], mix[:, 256:1280])):
-            cast_wa(nc.scalar.copy, region.bitcast(BF16), raw[a])
-            quantize(wa_w[1][a][:], wa_s[1][a][:], region.bitcast(BF16))
+        for jb in range(4):
+            for a in range(2):
+                product_b(banks[jb % 2], 1, jb, a)
+            tanh_b(banks[jb % 2], 1, jb)
+        pair = keep.tile([P, 5 * PICK], F32, name="pair", tag="wb_w1", align_bytes=64)
+        for t in range(2):
+            picked[t] = pair[:, PICK * t : PICK * (t + 1)]
+            fetch(t)
+        load_page(4)
+        shared = [pair[:, PICK * u : PICK * (u + 1)] for u in range(2, 5)]
+        make_wc(1, shared[0].bitcast(BF16), raw[3], nc.scalar.copy)
+        make_wa(1, 0, shared[1].bitcast(BF16), raw[0], nc.scalar.copy)
+        make_wa(1, 1, shared[2].bitcast(BF16), raw[1], nc.scalar.copy)
+        h1.extend([shared[0][:, S:], shared[2][:, :S]])
         for t in range(2, PACK):
             mismatch(0, t)
-        fetch(0)
-        fetch(1)
-        load_page(4)
-        for t in range(2, PACK):
             put_line(t)
             fetch(t)
-        load_page(5)
+            load_page(t + 3)
+        late["planes"] = keep.tile([P, PICK * PACK], BF16, name="planes", tag="page0", align_bytes=64)
+        for t in range(2):
+            compress(t)
         for t in range(PACK):
             barcode(1, t)
         reading_a(1)
         for t in range(PACK):
             mismatch(1, t)
-        late["planes"] = keep.tile([P, PICK * PACK], BF16, name="planes", tag="page0", align_bytes=64)
         for h in range(2):
             x_bf.append(keep.tile([P, PICK * PACK], BF16, name="x_bf%d" % h, tag="tab_w%d" % h, align_bytes=64))
-        for t in range(PACK):
+        for t in range(2, PACK):
             compress(t)
-        weave()
+        weave(0, PACK)
         for i in range(4, 7):
             put_barcode(i)
             put_line(i)
             fetch(i)
             compress(i)
-            if i + 2 < 8:
-                load_page(i + 2)
+            if i == 4:
+                load_page(7)
+        weave(1, PACK - 1)
         quantize(x_w[0][:], x_s[0][:], x_bf[0][:])
         put_barcode(7)
         put_line(7)
@@ -339,21 +389,26 @@ def tile_list_reject_desk_scores_kernel(
             score(s, 0)
         ring = x_bf[0][:].bitcast(F32)
 
-        def finish(s):
-            cols = slice(SL * s, SL * (s + 1))
-            last = ring[:, cols]
-            gather(last, pages[page_of[7]][:], list5[:, SL // 16 * s : SL // 16 * (s + 1)])
-            nc.scalar.activation(last, last, ACT.Abs)
-            nc.scalar.activation(last, last, ACT.Ln, bias=1.0)
-            nc.vector.tensor_scalar(woven(1, 3, cols), last, gains[:, 7:8], None, MULT)
-            quantize(x_w[1][:, cols], x_s[1][:, cols], x_bf[1][:, PACK * SL * s : PACK * SL * (s + 1)])
-            score(s, 1)
+        slices = [slice(SL * s, SL * (s + 1)) for s in range(NS)]
+        for s in range(NS):
+            gather(ring[:, slices[s]], pages[page_of[7]][:], list5[:, SL // 16 * s : SL // 16 * (s + 1)])
+        for both in ((0, 1), (2, 3)):
+            for s in both:
+                nc.scalar.activation(ring[:, slices[s]], ring[:, slices[s]], ACT.Abs)
+            for s in both:
+                nc.scalar.activation(ring[:, slices[s]], ring[:, slices[s]], ACT.Ln, bias=1.0)
+            for s in both:
+                nc.vector.tensor_scalar(woven(1, 3, slices[s]), ring[:, slices[s]], gains[:, 7:8], None, MULT)
+            for s in both:
+                cols = slices[s]
+                quantize(x_w[1][:, cols], x_s[1][:, cols], x_bf[1][:, PACK * SL * s : PACK * SL * (s + 1)])
+                score(s, 1)
 
         def store(s):
             cols = slice(SL * s, SL * (s + 1))
             for u in range(2):
                 staged = raw[s][:, 512 * u : 512 * (u + 1)]
-                if u == 0 and s >= NS - 2:
+                if u == 0 and s == NS - 1:
                     nc.vector.tensor_copy(staged, banks[2 * s + u][:])
                 else:
                     nc.scalar.copy(staged, banks[2 * s + u][:])
@@ -362,7 +417,5 @@ def tile_list_reject_desk_scores_kernel(
                     in_=staged.rearrange("p (n c) -> p n c", n=2),
                 )
 
-        for s in range(NS):
-            finish(s)
         for s in range(NS):
             store(s)

@@ -55,8 +55,8 @@ def tile_list_reject_desk_scores_kernel(
         wb_s = [sb("wb_s%d" % h, [P, 2 * KP], U8) for h in range(2)]
         wo_w = sb("wo_w", [P, 2 * N], U32)
         wo_s = sb("wo_s", [P, 2 * N], U8)
-        bias = sb("bias", [P, 8], F32)
-        gains = sb("gains", [P, 8], F32)
+        bias = [sb("bias%d" % h, [P, PACK], F32) for h in range(2)]
+        gains = [sb("gains%d" % h, [P, PACK], F32) for h in range(2)]
         ident = sb("ident", [P, P], F32)
         wg1_n = sb("wg1_n", [P, S], F32)
         wg2_n = sb("wg2_n", [P, S], F32)
@@ -102,15 +102,17 @@ def tile_list_reject_desk_scores_kernel(
 
         def turn_gate(natural):
             for jb in range(4):
-                cols = slice(P * jb, P * (jb + 1))
-                nc.tensor.transpose(banks[6][:, cols], natural[:, cols], ident[:])
+                dst = banks[2 + jb // 2][:, P * (jb % 2) : P * (jb % 2 + 1)]
+                nc.tensor.transpose(dst, natural[:, P * jb : P * (jb + 1)], ident[:])
 
-        def deal_gate(dst, t, bank):
-            rows = banks[6][:].rearrange("p (jb m t) -> p jb m t", jb=4, t=PACK)[:, :, :, t]
-            nc.scalar.copy(
-                turned[t % 2][:].rearrange("p (jb q m) -> p jb q m", jb=4, q=4),
-                rows.unsqueeze(2).to_broadcast([P, 4, 4, 32]),
-            )
+        def deal_gate(dst, t):
+            bank = banks[t % 2]
+            for u in range(2):
+                rows = banks[2 + u][:, : 2 * P].rearrange("p (jb m t) -> p jb m t", jb=2, t=PACK)[:, :, :, t]
+                nc.scalar.copy(
+                    turned[t % 2][:, 2 * P * u : 2 * P * (u + 1)].rearrange("p (jb q m) -> p jb q m", jb=2, q=4),
+                    rows.unsqueeze(2).to_broadcast([P, 2, 4, 32]),
+                )
             for jb in range(4):
                 cols = slice(P * jb, P * (jb + 1))
                 nc.tensor.transpose(bank[:, cols], turned[t % 2][:, cols], ident[:])
@@ -135,14 +137,16 @@ def tile_list_reject_desk_scores_kernel(
         def quantize(words, scales, src):
             nc.vector.quantize_mx(out=words.bitcast(FP8X4), scales=scales, in_=src)
 
-        def make_wc(h, staged, src, copy):
-            for u in range(2):
+        def cast_wc(u, staged, src, copy):
+            if True:
                 half = staged[:, 1024 * u : 1024 * (u + 1)]
                 copy(
                     half.rearrange("p (t m i) -> p m i t", t=2, i=PACK),
                     src[:].rearrange("p (i m t) -> p m i t", i=PACK, t=PACK)[:, :, :, 2 * u : 2 * u + 2],
                 )
-            for u in range(2):
+
+        def quantize_wc(h, u, staged):
+            if True:
                 half = staged[:, 1024 * u : 1024 * (u + 1)]
                 quantize(wc_w[h][:, 256 * u : 256 * (u + 1)], wc_s[h][:, 256 * u : 256 * (u + 1)], half)
 
@@ -153,17 +157,18 @@ def tile_list_reject_desk_scores_kernel(
                     staged.rearrange("p (c e i) -> p c i e", e=4, i=PACK)[:, c],
                     src[:].rearrange("p (i c e) -> p c i e", i=PACK, e=4)[:, c],
                 )
-            quantize(wa_w[h][a][:], wa_s[h][a][:], staged)
+            for u in range(2):
+                cols = slice(256 * u, 256 * (u + 1))
+                quantize(wa_w[h][a][:, cols], wa_s[h][a][:, cols], staged[:, 1024 * u : 1024 * (u + 1)])
 
         def barcode(h, t):
-            bank = banks[(4, 2)[h] + t % 2]
+            bank = banks[4 + t % 2] if h == 0 else banks[(2 + t) % 4]
             cols = slice(P * t, P * (t + 1))
             nc.tensor.matmul_mx(
                 out=bank[:], lhsT=wc_w[h][:, cols].bitcast(FP8X4), lhsT_scale=wc_s[h][:, cols],
                 rhs=v2_w[:].bitcast(FP8X4), rhs_scale=v2_s[:], start=True, stop=True,
             )
-            i = PACK * h + t
-            nc.scalar.activation(h2[t][:], bank[:], ACT.Identity, bias=bias[:, i : i + 1])
+            nc.scalar.activation(h2[t][:], bank[:], ACT.Identity, bias=bias[h][:, t : t + 1])
 
         def line_product(bank, jb, a, rhs, rhs_scale):
             cols = slice(P * jb, P * (jb + 1))
@@ -230,11 +235,11 @@ def tile_list_reject_desk_scores_kernel(
                 nc.scalar.activation(picked[i][:, c], picked[i][:, c], ACT.Ln, bias=1.0)
             for c in halves:
                 dst = late["planes"][:, PICK * t : PICK * (t + 1)][:, c]
-                nc.scalar.activation(dst, picked[i][:, c], ACT.Copy, scale=gains[:, i : i + 1])
+                nc.scalar.activation(dst, picked[i][:, c], ACT.Copy, scale=gains[i // PACK][:, t : t + 1])
 
-        def weave(h, count):
-            for u in range(2):
-                c = slice(P * u, P * (u + 1))
+        def weave(h, count, pieces):
+            for u in range(pieces):
+                c = slice(2 * P // pieces * u, 2 * P // pieces * (u + 1))
                 nc.scalar.copy(
                     x_bf[h][:].rearrange("p (c e t) -> p c t e", e=4, t=PACK)[:, c, :count, :],
                     late["planes"][:].rearrange("p (t c e) -> p c t e", t=PACK, e=4)[:, c, :count, :],
@@ -259,9 +264,9 @@ def tile_list_reject_desk_scores_kernel(
         nc.scalar.activation(warm[:], warm[:], ACT.Tanh)
         make_identity(nc, ident[:])
 
-        def load_column(dst, vec):
+        def load_column(dst, vec, h):
             nc.sync.dma_start(
-                out=dst[:].rearrange("p (h t) -> p h t", t=PACK), in_=vec.rearrange("(h p t) -> p h t", h=2, t=PACK)
+                out=dst[h][:], in_=vec[KP * h : KP * (h + 1)].rearrange("(p t) -> p t", t=PACK)
             )
 
         def load_wb(h):
@@ -279,65 +284,74 @@ def tile_list_reject_desk_scores_kernel(
         load_words(tab2_w, tab2_words[0])
         load_raw(raw[0], wc, 0, 0)
         nc.sync.dma_start(list4[:], offs4)
-        load_column(bias, bc)
+        load_column(bias, bc, 0)
         load_scales(tab2_s, tab2_scales, (0, 2, 1, 3))
         load_page(0)
+        nc.sync.dma_start(out=wg1_n[:], in_=wg1)
         gather(v_rows[:], tab_s[:], list1[:])
-        for q in range(4):
+        for q in range(3):
             move_scales(0, q)
         load_words(tab_w[0], tab_words[0])
-        nc.sync.dma_start(out=wg1_n[:], in_=wg1)
+        move_scales(0, 3)
         for q in range(2):
             move_scales(1, q)
-        load_words(tab_w[1], tab_words[1])
+        load_page(1)
         for q in range(2, 4):
             move_scales(1, q)
         load_scales(wb_s[0], wb_scales[:, :, :KP], (0, 2))
+        load_words(tab_w[1], tab_words[1])
         load_raw(raw[1], wa, 0, 0)
         load_scales(wb_s[0], wb_scales[:, :, :KP], (1, 3))
-        load_wb(0)
-        load_page(1)
         load_raw(raw[2], wa, 1, 0)
+        load_wb(0)
         load_page(2)
-        nc.sync.dma_start(list3[:], offs3)
         load_page(3)
+        nc.sync.dma_start(list3[:], offs3)
         load_wb(1)
         load_scales(wb_s[1], wb_scales[:, :, KP:], (0, 2, 1, 3))
         nc.sync.dma_start(list5[:], offs5)
-        load_column(gains, gain)
+        load_column(gains, gain, 0)
         load_raw(raw[3], wc, 0, 1)
         gather(v2_w[:], tab2_w[:], list2[:])
 
         turn_gate(wg2_n)
-        deal_gate(wg2_d[0], 0, banks[0])
-        make_wc(0, stage[0][:], raw[0], nc.vector.tensor_copy)
+        for t in range(2):
+            deal_gate(wg2_d[t], t)
+        cast_wc(0, stage[0][:], raw[0], nc.vector.tensor_copy)
         gather(v2_s[:], tab2_s[:], list2[:])
-        load_raw(raw[0], wa, 0, 1)
-        barcode(0, 0)
+        quantize_wc(0, 0, stage[0][:])
+        cast_wc(1, stage[0][:], raw[0], nc.scalar.copy)
+        for t in range(2):
+            barcode(0, t)
         put_barcode(0)
-        for t in range(1, PACK):
-            deal_gate(wg2_d[t], t, banks[t])
+        quantize_wc(0, 1, stage[0][:])
+        load_raw(raw[0], wa, 0, 1)
+        for t in range(2, PACK):
+            deal_gate(wg2_d[t], t)
             barcode(0, t)
         turn_gate(wg1_n)
         gather(v_w[0][:], tab_w[0][:], list1[:])
+        put_barcode(1)
         gather(v_w[1][:], tab_w[1][:], list1[:])
         for t in range(PACK):
-            deal_gate(wg1_d[t], t, banks[4 + t % 2])
+            deal_gate(wg1_d[t], t)
         for a in range(2):
             for jb in range(4):
                 product_b(banks[jb], 0, jb, a)
-        for jb in range(4):
-            tanh_b(banks[jb], 0, jb)
         make_wa(0, 0, stage[1][:], raw[1], nc.vector.tensor_copy)
         make_wa(0, 1, stage[0][:], raw[2], nc.vector.tensor_copy)
+        for jb in range(4):
+            tanh_b(banks[jb], 0, jb)
         load_raw(raw[1], wa, 1, 1)
+        load_column(bias, bc, 1)
+        load_column(gains, gain, 1)
         load_scales(wo_s, wo_scales, range(4))
         nc.sync.dma_start(
             out=wo_w[:].bitcast(I32).rearrange("p (a c) -> p a c", a=2),
             in_=wo_words.rearrange("a p c i -> p a (c i)").bitcast(I32),
         )
         reading_a(0)
-        for t in range(1, PACK):
+        for t in range(2, PACK):
             put_barcode(t)
         for t in range(2):
             mismatch(0, t)
@@ -347,18 +361,22 @@ def tile_list_reject_desk_scores_kernel(
                 product_b(banks[jb % 2], 1, jb, a)
             tanh_b(banks[jb % 2], 1, jb)
         pair = keep.tile([P, 5 * PICK], F32, name="pair", tag="wb_w1", align_bytes=64)
-        for t in range(2):
-            picked[t] = pair[:, PICK * t : PICK * (t + 1)]
-            fetch(t)
+        picked[0] = pair[:, :PICK]
+        fetch(0)
+        for u in range(2):
+            cast_wc(u, pair[:, PICK : 2 * PICK].bitcast(BF16), raw[3], nc.scalar.copy)
+        for u in range(2):
+            quantize_wc(1, u, pair[:, PICK : 2 * PICK].bitcast(BF16))
+        make_wa(1, 0, pair[:, 2304:3328].bitcast(BF16), raw[0], nc.scalar.copy)
+        h1.extend([pair[:, 2048:2560], pair[:, 2560:3072]])
+        picked[1] = pair[:, 3072:4096]
+        fetch(1)
         load_page(4)
-        shared = [pair[:, PICK * u : PICK * (u + 1)] for u in range(2, 5)]
-        make_wc(1, shared[0].bitcast(BF16), raw[3], nc.scalar.copy)
-        make_wa(1, 0, shared[1].bitcast(BF16), raw[0], nc.scalar.copy)
-        make_wa(1, 1, shared[2].bitcast(BF16), raw[1], nc.scalar.copy)
-        h1.extend([shared[0][:, S:], shared[2][:, :S]])
         for t in range(2, PACK):
             mismatch(0, t)
             put_line(t)
+        make_wa(1, 1, pair[:, 4096:5120].bitcast(BF16), raw[1], nc.scalar.copy)
+        for t in range(2, PACK):
             fetch(t)
             load_page(t + 3)
         late["planes"] = keep.tile([P, PICK * PACK], BF16, name="planes", tag="page0", align_bytes=64)
@@ -373,21 +391,26 @@ def tile_list_reject_desk_scores_kernel(
             x_bf.append(keep.tile([P, PICK * PACK], BF16, name="x_bf%d" % h, tag="tab_w%d" % h, align_bytes=64))
         for t in range(2, PACK):
             compress(t)
-        weave(0, PACK)
+        weave(0, PACK, 2)
         for i in range(4, 7):
             put_barcode(i)
-            put_line(i)
+        put_line(4)
+        put_line(5)
+        for i in range(4, 7):
+            if i == 6:
+                put_line(i)
             fetch(i)
             compress(i)
             if i == 4:
                 load_page(7)
-        weave(1, PACK - 1)
-        quantize(x_w[0][:], x_s[0][:], x_bf[0][:])
+        weave(1, PACK - 1, 2)
+        for lo, hi in ((0, SL), (SL, 3 * SL), (3 * SL, PICK)):
+            quantize(x_w[0][:, lo:hi], x_s[0][:, lo:hi], x_bf[0][:, PACK * lo : PACK * hi])
         put_barcode(7)
         put_line(7)
         for s in range(NS):
             score(s, 0)
-        ring = x_bf[0][:].bitcast(F32)
+        ring = x_bf[0][:, PACK * SL : PACK * 3 * SL].bitcast(F32)
 
         slices = [slice(SL * s, SL * (s + 1)) for s in range(NS)]
         for s in range(NS):
@@ -398,7 +421,7 @@ def tile_list_reject_desk_scores_kernel(
             for s in both:
                 nc.scalar.activation(ring[:, slices[s]], ring[:, slices[s]], ACT.Ln, bias=1.0)
             for s in both:
-                nc.vector.tensor_scalar(woven(1, 3, slices[s]), ring[:, slices[s]], gains[:, 7:8], None, MULT)
+                nc.vector.tensor_scalar(woven(1, 3, slices[s]), ring[:, slices[s]], gains[1][:, 3:4], None, MULT)
             for s in both:
                 cols = slices[s]
                 quantize(x_w[1][:, cols], x_s[1][:, cols], x_bf[1][:, PACK * SL * s : PACK * SL * (s + 1)])
@@ -412,9 +435,15 @@ def tile_list_reject_desk_scores_kernel(
                     nc.vector.tensor_copy(staged, banks[2 * s + u][:])
                 else:
                     nc.scalar.copy(staged, banks[2 * s + u][:])
+                if s < NS - 1:
+                    nc.sync.dma_start(
+                        out=out[2 * P * u : 2 * P * (u + 1), cols].rearrange("(n p) c -> p n c", p=P),
+                        in_=staged.rearrange("p (n c) -> p n c", n=2),
+                    )
+            if s == NS - 1:
                 nc.sync.dma_start(
-                    out=out[2 * P * u : 2 * P * (u + 1), cols].rearrange("(n p) c -> p n c", p=P),
-                    in_=staged.rearrange("p (n c) -> p n c", n=2),
+                    out=out[:, cols].rearrange("(n p) c -> p n c", p=P),
+                    in_=raw[s][:, :1024].rearrange("p (n c) -> p n c", n=4),
                 )
 
         for s in range(NS):

@@ -20,8 +20,13 @@ MULT = mybir.AluOpType.mult
 P = 128
 PACK = 4
 KP = P * PACK
-SL = 256
-NS = PICK // SL
+BANK = 512
+BLOCKS = S // P
+QUADS = P // 32
+LAST = 2 * PACK - 1
+SLICE = 256
+SLICES = PICK // SLICE
+PAGE_BUFFER = (0, 1, 2, 3, 1, 2, 4, 1)
 
 
 def tile_list_reject_desk_scores_kernel(
@@ -33,10 +38,10 @@ def tile_list_reject_desk_scores_kernel(
         keep = ctx.enter_context(tc.tile_pool(name="keep", bufs=1))
         psum = ctx.enter_context(tc.psum_pool(name="psum", bufs=1))
 
-        def sb(name, shape, dtype):
-            return keep.tile(shape, dtype, name=name, align_bytes=64)
+        def sb(name, shape, dtype, over=None):
+            return keep.tile(shape, dtype, name=name, tag=over or name, align_bytes=64)
 
-        banks = [psum.tile([P, 512], F32, name="bank%d" % b) for b in range(8)]
+        banks = [psum.tile([P, BANK], F32, name="bank%d" % b) for b in range(8)]
         list1 = sb("list1", [P, S // 16], U16)
         list2 = sb("list2", [P, S // 16], U16)
         list3 = sb("list3", [P, S // 16], U16)
@@ -51,48 +56,54 @@ def tile_list_reject_desk_scores_kernel(
         v_s = [sb("v_s%d" % a, [P, S], U8) for a in range(2)]
         v2_w = sb("v2_w", [P, S], U32)
         v2_s = sb("v2_s", [P, S], U8)
-        wb_w = [sb("wb_w0", [P, 4 * KP], U8)[:], sb("wb_w1", [P, 20 * H], U8)[:, : 4 * KP]]
+        wb_w = [sb("wb_w0", [P, 4 * KP], U8)[:], sb("wb_w1", [P, 6 * PICK * 4], U8)[:, : 4 * KP]]
         wb_s = [sb("wb_s%d" % h, [P, 2 * KP], U8) for h in range(2)]
         wo_w = sb("wo_w", [P, 2 * N], U32)
         wo_s = sb("wo_s", [P, 2 * N], U8)
         bias = [sb("bias%d" % h, [P, PACK], F32) for h in range(2)]
         gains = [sb("gains%d" % h, [P, PACK], F32) for h in range(2)]
         ident = sb("ident", [P, P], F32)
-        wg1_n = sb("wg1_n", [P, S], F32)
-        wg2_n = sb("wg2_n", [P, S], F32)
+        wg1_rows = sb("wg1_rows", [P, S], F32)
+        wg2_rows = sb("wg2_rows", [P, S], F32)
         turned = [sb("turned%d" % u, [P, S], F32) for u in range(2)]
-        wg1_d = [sb("wg1_d%d" % t, [P, S], F32) for t in range(PACK)]
-        wg2_d = [sb("wg2_d%d" % t, [P, S], F32) for t in range(PACK)]
-        pages = [sb("page%d" % i, [P, T2], F32) for i in range(4)]
-        raw = [sb("raw%d" % i, [P, PACK * KP], F32) for i in range(4)]
-        stage = [sb("stage%d" % i, [P, PACK * KP], BF16) for i in range(2)]
+        gate1 = [sb("gate1_%d" % t, [P, S], F32) for t in range(PACK)]
+        gate2 = [sb("gate2_%d" % t, [P, S], F32) for t in range(PACK)]
+        pages = [sb("page%d" % b, [P, T2], F32) for b in range(max(PAGE_BUFFER) + 1)]
+        raw = [sb("raw%d" % b, [P, PACK * KP], F32) for b in range(4)]
+        stage = [sb("stage%d" % b, [P, PACK * KP], BF16) for b in range(2)]
         wc_w = [sb("wc_w%d" % h, [P, KP], U32) for h in range(2)]
         wc_s = [sb("wc_s%d" % h, [P, KP], U8) for h in range(2)]
         wa_w = [[sb("wa_w%d%d" % (h, a), [P, KP], U32) for a in range(2)] for h in range(2)]
         wa_s = [[sb("wa_s%d%d" % (h, a), [P, KP], U8) for a in range(2)] for h in range(2)]
-        ntanh = [[sb("ntanh%d%d" % (h, jb), [P, KP], F32) for jb in range(4)] for h in range(2)]
-        a_t = [sb("a_t%d" % jb, [P, KP], F32) for jb in range(4)]
-        h1 = [sb("h1_%d" % t, [P, S], F32)[:] for t in range(2)]
-        h2 = [sb("h2_%d" % t, [P, S], F32) for t in range(4)]
-        picked = {t: sb("picked%d" % t, [P, PICK], F32)[:] for t in (2, 3)}
-        for t in range(3):
-            picked[4 + t] = raw[t][:, PICK:]
-        warm = sb("warm", [P, 1], F32)
-        late = {}
+        minus_tanh = [[sb("minus_tanh%d%d" % (h, jb), [P, KP], F32) for jb in range(BLOCKS)] for h in range(2)]
+        reading = [sb("reading%d" % jb, [P, KP], F32) for jb in range(BLOCKS)]
+        h1 = [sb("h1_%d" % t, [P, S], F32) for t in range(PACK)]
+        h2 = [sb("h2_%d" % t, [P, S], F32) for t in range(PACK)]
         x_w = [sb("x_w%d" % h, [P, PICK], U32) for h in range(2)]
-        x_bf = []
         x_s = [sb("x_s%d" % h, [P, PICK], U8) for h in range(2)]
 
         def load_scales(dst, src, quadrants):
-            passes = src.shape[0]
             for q in quadrants:
                 nc.sync.dma_start(
-                    out=dst[32 * q : 32 * q + 4, :].bitcast(I32).rearrange("p (a c) -> p a c", a=passes),
+                    out=dst[32 * q : 32 * q + 4, :].bitcast(I32).rearrange("p (a c) -> p a c", a=src.shape[0]),
                     in_=src[:, 4 * q : 4 * q + 4, :].bitcast(I32).rearrange("a r c -> r a c"),
+                )
+
+        def move_scales(a, quadrants):
+            for q in quadrants:
+                first = 16 * a + 4 * q
+                nc.sync.dma_start(
+                    out=v_s[a][32 * q : 32 * q + 4, :].bitcast(I32), in_=v_rows[first : first + 4, :].bitcast(I32)
                 )
 
         def load_words(dst, src):
             nc.sync.dma_start(out=dst[:].bitcast(I32), in_=src.rearrange("p c i -> p (c i)").bitcast(I32))
+
+        def load_wb(h):
+            nc.sync.dma_start(
+                out=wb_w[h].bitcast(I32).rearrange("p (a c) -> p a c", a=2),
+                in_=wb_words[:, :, 2 * KP * h : 2 * KP * (h + 1)].bitcast(I32).rearrange("a p c -> p a c"),
+            )
 
         def load_raw(dst, w, a, h):
             nc.sync.dma_start(
@@ -100,75 +111,61 @@ def tile_list_reject_desk_scores_kernel(
                 in_=w[KP * a : KP * (a + 1), KP * h : KP * (h + 1)].rearrange("(p i) c -> p i c", i=PACK),
             )
 
-        def turn_gate(natural):
-            for jb in range(4):
-                dst = banks[2 + jb // 2][:, P * (jb % 2) : P * (jb % 2 + 1)]
-                nc.tensor.transpose(dst, natural[:, P * jb : P * (jb + 1)], ident[:])
-
-        def deal_gate(dst, t):
-            bank = banks[t % 2]
-            for u in range(2):
-                rows = banks[2 + u][:, : 2 * P].rearrange("p (jb m t) -> p jb m t", jb=2, t=PACK)[:, :, :, t]
-                nc.scalar.copy(
-                    turned[t % 2][:, 2 * P * u : 2 * P * (u + 1)].rearrange("p (jb q m) -> p jb q m", jb=2, q=4),
-                    rows.unsqueeze(2).to_broadcast([P, 2, 4, 32]),
-                )
-            for jb in range(4):
-                cols = slice(P * jb, P * (jb + 1))
-                nc.tensor.transpose(bank[:, cols], turned[t % 2][:, cols], ident[:])
-            nc.scalar.copy(dst[:], bank[:])
-
-        def move_scales(a, q):
-            first = 16 * a + 4 * q
-            nc.sync.dma_start(
-                out=v_s[a][32 * q : 32 * q + 4, :].bitcast(I32), in_=v_rows[first : first + 4, :].bitcast(I32)
-            )
-
-        page_of = [0, 1, 2, 3, 1, 2, 3, 1]
+        def load_per_row(dst, vec, h):
+            nc.sync.dma_start(out=dst[h][:], in_=vec[KP * h : KP * (h + 1)].rearrange("(p t) -> p t", t=PACK))
 
         def load_page(i):
             h, t = divmod(i, PACK)
             rows = page0[KP * h : KP * (h + 1), :].rearrange("(p t) c -> p t c", t=PACK)
-            nc.sync.dma_start(out=pages[page_of[i]][:], in_=rows[:, t, :])
+            nc.sync.dma_start(out=pages[PAGE_BUFFER[i]][:], in_=rows[:, t, :])
 
         def gather(dst, window, offsets):
             nc.vector.tensor_copy(dst, window.indirect(offsets))
 
-        def quantize(words, scales, src):
-            nc.vector.quantize_mx(out=words.bitcast(FP8X4), scales=scales, in_=src)
+        def quantize(words, scales, woven, first, last):
+            nc.vector.quantize_mx(
+                out=words[:, first:last].bitcast(FP8X4), scales=scales[:, first:last],
+                in_=woven[:, PACK * first : PACK * last],
+            )
 
-        def cast_wc(u, staged, src, copy):
-            if True:
-                half = staged[:, 1024 * u : 1024 * (u + 1)]
-                copy(
-                    half.rearrange("p (t m i) -> p m i t", t=2, i=PACK),
-                    src[:].rearrange("p (i m t) -> p m i t", i=PACK, t=PACK)[:, :, :, 2 * u : 2 * u + 2],
-                )
+        def turn_gate(rows):
+            for jb in range(BLOCKS):
+                dst = banks[2 + jb // 2][:, P * (jb % 2) : P * (jb % 2 + 1)]
+                nc.tensor.transpose(dst, rows[:, P * jb : P * (jb + 1)], ident[:])
 
-        def quantize_wc(h, u, staged):
-            if True:
-                half = staged[:, 1024 * u : 1024 * (u + 1)]
-                quantize(wc_w[h][:, 256 * u : 256 * (u + 1)], wc_s[h][:, 256 * u : 256 * (u + 1)], half)
-
-        def make_wa(h, a, staged, src, copy):
+        def deal_gate(dst, t):
             for u in range(2):
-                c = slice(64 * u, 64 * (u + 1))
-                copy(
-                    staged.rearrange("p (c e i) -> p c i e", e=4, i=PACK)[:, c],
-                    src[:].rearrange("p (i c e) -> p c i e", i=PACK, e=4)[:, c],
+                rows = banks[2 + u][:, : 2 * P].rearrange("p (jb m t) -> p jb m t", jb=2, t=PACK)[:, :, :, t]
+                nc.scalar.copy(
+                    turned[t % 2][:, 2 * P * u : 2 * P * (u + 1)].rearrange("p (jb q m) -> p jb q m", jb=2, q=QUADS),
+                    rows.unsqueeze(2).to_broadcast([P, 2, QUADS, 32]),
                 )
+            for jb in range(BLOCKS):
+                cols = slice(P * jb, P * (jb + 1))
+                nc.tensor.transpose(banks[t % 2][:, cols], turned[t % 2][:, cols], ident[:])
+            nc.scalar.copy(dst[:], banks[t % 2][:])
+
+        def round_wc(u, woven, src, copy):
+            copy(
+                woven[:, PICK * u : PICK * (u + 1)].rearrange("p (t m i) -> p m i t", t=2, i=PACK),
+                src[:].rearrange("p (i m t) -> p m i t", i=PACK, t=PACK)[:, :, :, 2 * u : 2 * u + 2],
+            )
+
+        def round_wa(woven, src, copy):
             for u in range(2):
-                cols = slice(256 * u, 256 * (u + 1))
-                quantize(wa_w[h][a][:, cols], wa_s[h][a][:, cols], staged[:, 1024 * u : 1024 * (u + 1)])
+                part = slice(P // 2 * u, P // 2 * (u + 1))
+                copy(
+                    woven.rearrange("p (c e i) -> p c i e", e=4, i=PACK)[:, part],
+                    src[:].rearrange("p (i c e) -> p c i e", i=PACK, e=4)[:, part],
+                )
 
         def barcode(h, t):
-            bank = banks[4 + t % 2] if h == 0 else banks[(2 + t) % 4]
             cols = slice(P * t, P * (t + 1))
             nc.tensor.matmul_mx(
-                out=bank[:], lhsT=wc_w[h][:, cols].bitcast(FP8X4), lhsT_scale=wc_s[h][:, cols],
+                out=banks[4 + t][:], lhsT=wc_w[h][:, cols].bitcast(FP8X4), lhsT_scale=wc_s[h][:, cols],
                 rhs=v2_w[:].bitcast(FP8X4), rhs_scale=v2_s[:], start=True, stop=True,
             )
-            nc.scalar.activation(h2[t][:], bank[:], ACT.Identity, bias=bias[h][:, t : t + 1])
+            nc.scalar.activation(h2[t][:], banks[4 + t][:], ACT.Identity, bias=bias[h][:, t : t + 1])
 
         def line_product(bank, jb, a, rhs, rhs_scale):
             cols = slice(P * jb, P * (jb + 1))
@@ -177,274 +174,256 @@ def tile_list_reject_desk_scores_kernel(
                 rhs=rhs, rhs_scale=rhs_scale, start=(a == 0), stop=(a == 1),
             )
 
-        def dealt_in(bank):
+        def product_b(bank, h, jb, a):
+            words = wb_w[h][:, 2 * KP * a : 2 * KP * (a + 1)].bitcast(FP4X4)
+            line_product(bank, jb, a, words, wb_s[h][:, KP * a : KP * (a + 1)])
+
+        def by_tile_in(bank):
             return bank[:].rearrange("p (m t) -> p t m", t=PACK)
 
-        def dealt_out(dst):
+        def by_tile_out(dst):
             return dst[:].rearrange("p (t m) -> p t m", t=PACK)
 
-        def product_b(bank, h, jb, a):
-            line_product(
-                bank, jb, a, wb_w[h][:, 2 * KP * a : 2 * KP * (a + 1)].bitcast(FP4X4),
-                wb_s[h][:, KP * a : KP * (a + 1)],
-            )
-
         def tanh_b(bank, h, jb):
-            nc.scalar.activation(dealt_out(ntanh[h][jb]), dealt_in(bank), ACT.Tanh, scale=-1.0)
+            nc.scalar.activation(by_tile_out(minus_tanh[h][jb]), by_tile_in(bank), ACT.Tanh, scale=-1.0)
 
         def reading_a(h):
             for a in range(2):
-                for jb in range(4):
+                for jb in range(BLOCKS):
                     line_product(banks[4 + jb], jb, a, wa_w[h][a][:].bitcast(FP8X4), wa_s[h][a][:])
             for u in range(2):
-                for jb in range(4):
-                    pair = slice(2 * u, 2 * u + 2)
-                    nc.scalar.copy(dealt_out(a_t[jb])[:, pair, :], dealt_in(banks[4 + jb])[:, pair, :])
+                for jb in range(BLOCKS):
+                    tiles = slice(2 * u, 2 * u + 2)
+                    nc.scalar.copy(by_tile_out(reading[jb])[:, tiles, :], by_tile_in(banks[4 + jb])[:, tiles, :])
 
         def mismatch(h, t):
-            bank = banks[t % 2]
             cols = slice(P * t, P * (t + 1))
-            for jb in range(4):
-                dst = bank[:, P * jb : P * (jb + 1)]
-                nc.tensor.matmul(dst, a_t[jb][:, cols], ident[:], start=True, stop=False, is_transpose=True)
-                nc.tensor.matmul(dst, ntanh[h][jb][:, cols], ident[:], start=False, stop=True, is_transpose=True)
-            nc.scalar.activation(h1[t], bank[:], ACT.Square)
+            for jb in range(BLOCKS):
+                dst = banks[t % 2][:, P * jb : P * (jb + 1)]
+                nc.tensor.matmul(dst, reading[jb][:, cols], ident[:], start=True, stop=False, is_transpose=True)
+                nc.tensor.matmul(dst, minus_tanh[h][jb][:, cols], ident[:], start=False, stop=True, is_transpose=True)
+            nc.scalar.activation(h1[t][:], banks[t % 2][:], ACT.Square)
 
         def put_barcode(i):
-            t = i % PACK
-            gate = wg2_d[t][:]
-            nc.vector.tensor_tensor(pages[page_of[i]][:].indirect(list4[:]), h2[t][:], gate, MULT)
+            window = pages[PAGE_BUFFER[i]][:].indirect(list4[:])
+            nc.vector.tensor_tensor(window, h2[i % PACK][:], gate2[i % PACK][:], MULT)
 
         def put_line(i):
-            t = i % PACK
-            gate = wg1_d[t][:]
-            nc.vector.tensor_tensor(pages[page_of[i]][:].indirect(list3[:]), h1[t], gate, MULT)
+            window = pages[PAGE_BUFFER[i]][:].indirect(list3[:])
+            nc.vector.tensor_tensor(window, h1[i % PACK][:], gate1[i % PACK][:], MULT)
 
-        def woven(h, t, cols):
-            return x_bf[h][:].rearrange("p (j t) -> p j t", t=PACK)[:, cols, t]
+        def fetch(i, dst):
+            gather(dst, pages[PAGE_BUFFER[i]][:], list5[:])
 
-        def fetch(i):
-            gather(picked[i], pages[page_of[i]][:], list5[:])
+        def log_abs(pieces):
+            for piece in pieces:
+                nc.scalar.activation(piece, piece, ACT.Abs)
+            for piece in pieces:
+                nc.scalar.activation(piece, piece, ACT.Ln, bias=1.0)
 
-        def compress(i):
-            t = i % PACK
-            halves = [slice(S * u, S * (u + 1)) for u in range(2)]
-            for c in halves:
-                nc.scalar.activation(picked[i][:, c], picked[i][:, c], ACT.Abs)
-            for c in halves:
-                nc.scalar.activation(picked[i][:, c], picked[i][:, c], ACT.Ln, bias=1.0)
-            for c in halves:
-                dst = late["planes"][:, PICK * t : PICK * (t + 1)][:, c]
-                nc.scalar.activation(dst, picked[i][:, c], ACT.Copy, scale=gains[i // PACK][:, t : t + 1])
+        def compress(i, picked, x_rows):
+            h, t = divmod(i, PACK)
+            log_abs([picked[:, S * u : S * (u + 1)] for u in range(2)])
+            for u in range(2):
+                dst = x_rows[:, PICK * t + S * u : PICK * t + S * (u + 1)]
+                nc.scalar.activation(dst, picked[:, S * u : S * (u + 1)], ACT.Copy, scale=gains[h][:, t : t + 1])
 
-        def weave(h, count, pieces):
-            for u in range(pieces):
-                c = slice(2 * P // pieces * u, 2 * P // pieces * (u + 1))
+        def weave(woven, x_rows, tiles):
+            for u in range(2):
+                part = slice(P * u, P * (u + 1))
                 nc.scalar.copy(
-                    x_bf[h][:].rearrange("p (c e t) -> p c t e", e=4, t=PACK)[:, c, :count, :],
-                    late["planes"][:].rearrange("p (t c e) -> p c t e", t=PACK, e=4)[:, c, :count, :],
+                    woven[:].rearrange("p (c e t) -> p c t e", e=4, t=PACK)[:, part, :tiles, :],
+                    x_rows[:].rearrange("p (t c e) -> p c t e", t=PACK, e=4)[:, part, :tiles, :],
                 )
 
         def score(s, h):
-            cols = slice(SL * s, SL * (s + 1))
-            for n in range(4):
+            cols = slice(SLICE * s, SLICE * (s + 1))
+            for n in range(N // P):
+                wo_cols = slice(N * h + P * n, N * h + P * (n + 1))
                 nc.tensor.matmul_mx(
-                    out=banks[2 * s + n // 2][:, SL * (n % 2) : SL * (n % 2 + 1)],
-                    lhsT=wo_w[:, N * h + P * n : N * h + P * (n + 1)].bitcast(FP8X4),
-                    lhsT_scale=wo_s[:, N * h + P * n : N * h + P * (n + 1)],
+                    out=banks[2 * s + n // 2][:, SLICE * (n % 2) : SLICE * (n % 2 + 1)],
+                    lhsT=wo_w[:, wo_cols].bitcast(FP8X4), lhsT_scale=wo_s[:, wo_cols],
                     rhs=x_w[h][:, cols].bitcast(FP8X4), rhs_scale=x_s[h][:, cols],
                     start=(h == 0 and n % 2 == 0), stop=(h == 1 and n % 2 == 1),
                 )
 
+        def store(s, first, banks_stored):
+            nc.sync.dma_start(
+                out=out[2 * P * first : 2 * P * (first + banks_stored), SLICE * s : SLICE * (s + 1)].rearrange(
+                    "(n p) c -> p n c", p=P
+                ),
+                in_=raw[s][:, BANK * first : BANK * (first + banks_stored)].rearrange("p (n c) -> p n c", c=SLICE),
+            )
+
         for unused in (slice(32, 64), slice(64, P)):
             nc.vector.memset(tab_s[unused, :].bitcast(I32), 0)
-        for plane in (tab2_s, wb_s[0], v_s[0], v_s[1], wb_s[1], wo_s):
-            nc.vector.memset(plane[:].bitcast(I32), 0)
-        nc.vector.memset(warm[:], 0.0)
-        nc.scalar.activation(warm[:], warm[:], ACT.Tanh)
+        for scales in (tab2_s, wb_s[0], v_s[0], v_s[1], wb_s[1], wo_s):
+            nc.vector.memset(scales[:].bitcast(I32), 0)
         make_identity(nc, ident[:])
 
-        def load_column(dst, vec, h):
-            nc.sync.dma_start(
-                out=dst[h][:], in_=vec[KP * h : KP * (h + 1)].rearrange("(p t) -> p t", t=PACK)
-            )
-
-        def load_wb(h):
-            nc.sync.dma_start(
-                out=wb_w[h].bitcast(I32).rearrange("p (a c) -> p a c", a=2),
-                in_=wb_words[:, :, 2 * KP * h : 2 * KP * (h + 1)].bitcast(I32).rearrange("a p c -> p a c"),
-            )
-
-        nc.sync.dma_start(out=wg2_n[:], in_=wg2)
+        nc.sync.dma_start(out=wg2_rows[:], in_=wg2)
         nc.sync.dma_start(list1[:], offs)
-        nc.sync.dma_start(
-            out=tab_s[0:32, :].bitcast(I32), in_=tab_scales.rearrange("a r c -> (a r) c").bitcast(I32)
-        )
+        nc.sync.dma_start(out=tab_s[0:32, :].bitcast(I32), in_=tab_scales.rearrange("a r c -> (a r) c").bitcast(I32))
         nc.sync.dma_start(list2[:], offs2)
         load_words(tab2_w, tab2_words[0])
         load_raw(raw[0], wc, 0, 0)
         nc.sync.dma_start(list4[:], offs4)
-        load_column(bias, bc, 0)
+        load_per_row(bias, bc, 0)
         load_scales(tab2_s, tab2_scales, (0, 2, 1, 3))
         load_page(0)
-        nc.sync.dma_start(out=wg1_n[:], in_=wg1)
+        nc.sync.dma_start(out=wg1_rows[:], in_=wg1)
         gather(v_rows[:], tab_s[:], list1[:])
-        for q in range(3):
-            move_scales(0, q)
+        move_scales(0, (0, 1, 2))
         load_words(tab_w[0], tab_words[0])
-        move_scales(0, 3)
-        for q in range(2):
-            move_scales(1, q)
+        move_scales(0, (3,))
+        move_scales(1, (0, 1))
         load_page(1)
-        for q in range(2, 4):
-            move_scales(1, q)
+        move_scales(1, (2, 3))
         load_scales(wb_s[0], wb_scales[:, :, :KP], (0, 2))
         load_words(tab_w[1], tab_words[1])
-        load_raw(raw[1], wa, 0, 0)
         load_scales(wb_s[0], wb_scales[:, :, :KP], (1, 3))
-        load_raw(raw[2], wa, 1, 0)
         load_wb(0)
+        load_raw(raw[1], wa, 0, 0)
+        load_raw(raw[2], wa, 1, 0)
         load_page(2)
         load_page(3)
         nc.sync.dma_start(list3[:], offs3)
         load_wb(1)
         load_scales(wb_s[1], wb_scales[:, :, KP:], (0, 2, 1, 3))
         nc.sync.dma_start(list5[:], offs5)
-        load_column(gains, gain, 0)
+        load_per_row(gains, gain, 0)
         load_raw(raw[3], wc, 0, 1)
-        gather(v2_w[:], tab2_w[:], list2[:])
 
-        turn_gate(wg2_n)
+        gather(v2_w[:], tab2_w[:], list2[:])
+        turn_gate(wg2_rows)
         for t in range(2):
-            deal_gate(wg2_d[t], t)
-        cast_wc(0, stage[0][:], raw[0], nc.vector.tensor_copy)
+            deal_gate(gate2[t], t)
+        round_wc(0, stage[0], raw[0], nc.vector.tensor_copy)
         gather(v2_s[:], tab2_s[:], list2[:])
-        quantize_wc(0, 0, stage[0][:])
-        cast_wc(1, stage[0][:], raw[0], nc.scalar.copy)
+        quantize(wc_w[0], wc_s[0], stage[0], 0, KP // 2)
+        round_wc(1, stage[0], raw[0], nc.scalar.copy)
         for t in range(2):
             barcode(0, t)
         put_barcode(0)
-        quantize_wc(0, 1, stage[0][:])
+        quantize(wc_w[0], wc_s[0], stage[0], KP // 2, KP)
         load_raw(raw[0], wa, 0, 1)
         for t in range(2, PACK):
-            deal_gate(wg2_d[t], t)
+            deal_gate(gate2[t], t)
             barcode(0, t)
-        turn_gate(wg1_n)
+        turn_gate(wg1_rows)
         gather(v_w[0][:], tab_w[0][:], list1[:])
         put_barcode(1)
         gather(v_w[1][:], tab_w[1][:], list1[:])
         for t in range(PACK):
-            deal_gate(wg1_d[t], t)
+            deal_gate(gate1[t], t)
         for a in range(2):
-            for jb in range(4):
+            for jb in range(BLOCKS):
                 product_b(banks[jb], 0, jb, a)
-        make_wa(0, 0, stage[1][:], raw[1], nc.vector.tensor_copy)
-        make_wa(0, 1, stage[0][:], raw[2], nc.vector.tensor_copy)
-        for jb in range(4):
+        for a in range(2):
+            round_wa(stage[1 - a][:], raw[1 + a], nc.vector.tensor_copy)
+            for first in (0, KP // 2):
+                quantize(wa_w[0][a], wa_s[0][a], stage[1 - a], first, first + KP // 2)
+        for jb in range(BLOCKS):
             tanh_b(banks[jb], 0, jb)
         load_raw(raw[1], wa, 1, 1)
-        load_column(bias, bc, 1)
-        load_column(gains, gain, 1)
-        load_scales(wo_s, wo_scales, range(4))
+        load_per_row(bias, bc, 1)
+        load_per_row(gains, gain, 1)
+        load_scales(wo_s, wo_scales, range(QUADS))
         nc.sync.dma_start(
             out=wo_w[:].bitcast(I32).rearrange("p (a c) -> p a c", a=2),
             in_=wo_words.rearrange("a p c i -> p a (c i)").bitcast(I32),
         )
+        load_page(6)
         reading_a(0)
         for t in range(2, PACK):
             put_barcode(t)
-        for t in range(2):
+        for t in range(PACK):
             mismatch(0, t)
             put_line(t)
-        for jb in range(4):
+
+        for jb in range(BLOCKS):
             for a in range(2):
                 product_b(banks[jb % 2], 1, jb, a)
             tanh_b(banks[jb % 2], 1, jb)
-        pair = keep.tile([P, 5 * PICK], F32, name="pair", tag="wb_w1", align_bytes=64)
-        picked[0] = pair[:, :PICK]
-        fetch(0)
+
+        middle = sb("middle", [P, 6 * PICK], F32, over="wb_w1")
+        overlap = PICK // 4
+
+        def span(first):
+            return middle[:, first : first + PICK]
+
+        woven_wc = span(0).bitcast(BF16)
+        woven_wa = [span(2 * PICK - overlap).bitcast(BF16), span(4 * PICK + overlap).bitcast(BF16)]
+        picked = [span(PICK - overlap), span(3 * PICK - 2 * overlap), span(4 * PICK - 2 * overlap), span(5 * PICK)]
+        picked.extend(raw[t][:, PICK:] for t in range(PACK - 1))
+
         for u in range(2):
-            cast_wc(u, pair[:, PICK : 2 * PICK].bitcast(BF16), raw[3], nc.scalar.copy)
-        for u in range(2):
-            quantize_wc(1, u, pair[:, PICK : 2 * PICK].bitcast(BF16))
-        make_wa(1, 0, pair[:, 2304:3328].bitcast(BF16), raw[0], nc.scalar.copy)
-        h1.extend([pair[:, 2048:2560], pair[:, 2560:3072]])
-        picked[1] = pair[:, 3072:4096]
-        fetch(1)
+            round_wc(u, woven_wc, raw[3], nc.scalar.copy)
+        quantize(wc_w[1], wc_s[1], woven_wc, 0, KP)
+        fetch(0, picked[0])
+        round_wa(woven_wa[0], raw[0], nc.scalar.copy)
+        quantize(wa_w[1][0], wa_s[1][0], woven_wa[0], 0, KP)
+        fetch(1, picked[1])
         load_page(4)
-        for t in range(2, PACK):
-            mismatch(0, t)
-            put_line(t)
-        make_wa(1, 1, pair[:, 4096:5120].bitcast(BF16), raw[1], nc.scalar.copy)
-        for t in range(2, PACK):
-            fetch(t)
-            load_page(t + 3)
-        late["planes"] = keep.tile([P, PICK * PACK], BF16, name="planes", tag="page0", align_bytes=64)
-        for t in range(2):
-            compress(t)
+        round_wa(woven_wa[1], raw[1], nc.scalar.copy)
+        quantize(wa_w[1][1], wa_s[1][1], woven_wa[1], 0, KP)
+        fetch(2, picked[2])
+        load_page(5)
+        fetch(3, picked[3])
+
         for t in range(PACK):
             barcode(1, t)
+        x_rows = sb("x_rows", [P, PACK * PICK], BF16, over="page0")
+        for i in range(2):
+            compress(i, picked[i], x_rows)
         reading_a(1)
         for t in range(PACK):
             mismatch(1, t)
-        for h in range(2):
-            x_bf.append(keep.tile([P, PICK * PACK], BF16, name="x_bf%d" % h, tag="tab_w%d" % h, align_bytes=64))
-        for t in range(2, PACK):
-            compress(t)
-        weave(0, PACK, 2)
-        for i in range(4, 7):
+        woven_x = [sb("woven_x%d" % h, [P, PICK * PACK], BF16, over="tab_w%d" % h) for h in range(2)]
+        for i in range(2, PACK):
+            compress(i, picked[i], x_rows)
+        weave(woven_x[0], x_rows, PACK)
+
+        for i in range(PACK, LAST):
             put_barcode(i)
         put_line(4)
         put_line(5)
-        for i in range(4, 7):
-            if i == 6:
-                put_line(i)
-            fetch(i)
-            compress(i)
-            if i == 4:
-                load_page(7)
-        weave(1, PACK - 1, 2)
-        for lo, hi in ((0, SL), (SL, 3 * SL), (3 * SL, PICK)):
-            quantize(x_w[0][:, lo:hi], x_s[0][:, lo:hi], x_bf[0][:, PACK * lo : PACK * hi])
-        put_barcode(7)
-        put_line(7)
-        for s in range(NS):
-            score(s, 0)
-        ring = x_bf[0][:, PACK * SL : PACK * 3 * SL].bitcast(F32)
+        fetch(4, picked[4])
+        compress(4, picked[4], x_rows)
+        load_page(LAST)
+        fetch(5, picked[5])
+        compress(5, picked[5], x_rows)
+        put_line(6)
+        fetch(6, picked[6])
+        compress(6, picked[6], x_rows)
+        weave(woven_x[1], x_rows, PACK - 1)
 
-        slices = [slice(SL * s, SL * (s + 1)) for s in range(NS)]
-        for s in range(NS):
-            gather(ring[:, slices[s]], pages[page_of[7]][:], list5[:, SL // 16 * s : SL // 16 * (s + 1)])
-        for both in ((0, 1), (2, 3)):
-            for s in both:
-                nc.scalar.activation(ring[:, slices[s]], ring[:, slices[s]], ACT.Abs)
-            for s in both:
-                nc.scalar.activation(ring[:, slices[s]], ring[:, slices[s]], ACT.Ln, bias=1.0)
-            for s in both:
-                nc.vector.tensor_scalar(woven(1, 3, slices[s]), ring[:, slices[s]], gains[1][:, 3:4], None, MULT)
-            for s in both:
-                cols = slices[s]
-                quantize(x_w[1][:, cols], x_s[1][:, cols], x_bf[1][:, PACK * SL * s : PACK * SL * (s + 1)])
+        for first, last in ((0, SLICE), (SLICE, 3 * SLICE), (3 * SLICE, PICK)):
+            quantize(x_w[0], x_s[0], woven_x[0], first, last)
+        put_barcode(LAST)
+        put_line(LAST)
+        for s in range(SLICES):
+            score(s, 0)
+
+        tail = woven_x[0][:, PACK * SLICE : PACK * 3 * SLICE].bitcast(F32)
+        pieces = [tail[:, SLICE * s : SLICE * (s + 1)] for s in range(SLICES)]
+        last_place = woven_x[1][:].rearrange("p (j t) -> p j t", t=PACK)[:, :, PACK - 1]
+        for s in range(SLICES):
+            offsets = list5[:, SLICE // 16 * s : SLICE // 16 * (s + 1)]
+            gather(pieces[s], pages[PAGE_BUFFER[LAST]][:], offsets)
+        for s0 in range(0, SLICES, 2):
+            log_abs(pieces[s0 : s0 + 2])
+            for s in (s0, s0 + 1):
+                dst = last_place[:, SLICE * s : SLICE * (s + 1)]
+                nc.vector.tensor_scalar(dst, pieces[s], gains[1][:, PACK - 1 : PACK], None, MULT)
+            for s in (s0, s0 + 1):
+                quantize(x_w[1], x_s[1], woven_x[1], SLICE * s, SLICE * (s + 1))
                 score(s, 1)
 
-        def store(s):
-            cols = slice(SL * s, SL * (s + 1))
+        for s in range(SLICES - 1):
             for u in range(2):
-                staged = raw[s][:, 512 * u : 512 * (u + 1)]
-                if u == 0 and s == NS - 1:
-                    nc.vector.tensor_copy(staged, banks[2 * s + u][:])
-                else:
-                    nc.scalar.copy(staged, banks[2 * s + u][:])
-                if s < NS - 1:
-                    nc.sync.dma_start(
-                        out=out[2 * P * u : 2 * P * (u + 1), cols].rearrange("(n p) c -> p n c", p=P),
-                        in_=staged.rearrange("p (n c) -> p n c", n=2),
-                    )
-            if s == NS - 1:
-                nc.sync.dma_start(
-                    out=out[:, cols].rearrange("(n p) c -> p n c", p=P),
-                    in_=raw[s][:, :1024].rearrange("p (n c) -> p n c", n=4),
-                )
-
-        for s in range(NS):
-            store(s)
+                nc.scalar.copy(raw[s][:, BANK * u : BANK * (u + 1)], banks[2 * s + u][:])
+                store(s, u, 1)
+        nc.vector.tensor_copy(raw[SLICES - 1][:, :BANK], banks[2 * SLICES - 2][:])
+        nc.scalar.copy(raw[SLICES - 1][:, BANK : 2 * BANK], banks[2 * SLICES - 1][:])
+        store(SLICES - 1, 0, 2)

from contextlib import ExitStack

import concourse.mybir as mybir
from concourse.masks import make_identity

K, K2, H, N, T, TB, S, T2, PICK = 1024, 512, 1024, 512, 2048, 1024, 512, 2048, 1024
FLOPS = 2 * S * H * (2 * K + K2) + 2 * H * N * PICK

F32 = mybir.dt.float32
BF16 = mybir.dt.bfloat16
I32 = mybir.dt.int32
U32 = mybir.dt.uint32
U16 = mybir.dt.uint16
U8 = mybir.dt.uint8
FP8X4 = mybir.dt.float8_e4m3fn_x4
FP4X4 = mybir.dt.float4_e2m1fn_x4
ACT = mybir.ActivationFunctionType
MULT = mybir.AluOpType.mult

P = 128
PACK = 4
KP = P * PACK
BANK = 512
BLOCKS = S // P
QUADS = P // 32
LAST = 2 * PACK - 1
SLICE = 256
SLICES = PICK // SLICE
PAGE_BUFFER = (0, 1, 2, 3, 1, 2, 4, 1)


def tile_list_reject_desk_scores_kernel(
    tc, tab_words, tab_scales, tab2_words, tab2_scales, wa, wb_words, wb_scales, wc, bc, page0,
    wg1, wg2, gain, wo_words, wo_scales, offs, offs2, offs3, offs4, offs5, out,
):
    nc = tc.nc
    with ExitStack() as ctx:
        keep = ctx.enter_context(tc.tile_pool(name="keep", bufs=1))
        psum = ctx.enter_context(tc.psum_pool(name="psum", bufs=1))

        def sb(name, shape, dtype, over=None):
            return keep.tile(shape, dtype, name=name, tag=over or name, align_bytes=64)

        banks = [psum.tile([P, BANK], F32, name="bank%d" % b) for b in range(8)]
        list1 = sb("list1", [P, S // 16], U16)
        list2 = sb("list2", [P, S // 16], U16)
        list3 = sb("list3", [P, S // 16], U16)
        list4 = sb("list4", [P, S // 16], U16)
        list5 = sb("list5", [P, PICK // 16], U16)
        tab_w = [sb("tab_w%d" % a, [P, T], U32) for a in range(2)]
        tab_s = sb("tab_s", [P, T], U8)
        v_rows = sb("v_rows", [P, S], U8)
        tab2_w = sb("tab2_w", [P, TB], U32)
        tab2_s = sb("tab2_s", [P, TB], U8)
        v_w = [sb("v_w%d" % a, [P, S], U32) for a in range(2)]
        v_s = [sb("v_s%d" % a, [P, S], U8) for a in range(2)]
        v2_w = sb("v2_w", [P, S], U32)
        v2_s = sb("v2_s", [P, S], U8)
        wb_w = [sb("wb_w0", [P, 4 * KP], U8)[:], sb("wb_w1", [P, 6 * PICK * 4], U8)[:, : 4 * KP]]
        wb_s = [sb("wb_s%d" % h, [P, 2 * KP], U8) for h in range(2)]
        wo_w = sb("wo_w", [P, 2 * N], U32)
        wo_s = sb("wo_s", [P, 2 * N], U8)
        bias = [sb("bias%d" % h, [P, PACK], F32) for h in range(2)]
        gains = [sb("gains%d" % h, [P, PACK], F32) for h in range(2)]
        ident = sb("ident", [P, P], F32)
        wg1_rows = sb("wg1_rows", [P, S], F32)
        wg2_rows = sb("wg2_rows", [P, S], F32)
        turned = [sb("turned%d" % u, [P, S], F32) for u in range(2)]
        gate1 = [sb("gate1_%d" % t, [P, S], F32) for t in range(PACK)]
        gate2 = [sb("gate2_%d" % t, [P, S], F32) for t in range(PACK)]
        pages = [sb("page%d" % b, [P, T2], F32) for b in range(max(PAGE_BUFFER) + 1)]
        raw = [sb("raw%d" % b, [P, PACK * KP], F32) for b in range(4)]
        stage = [sb("stage%d" % b, [P, PACK * KP], BF16) for b in range(2)]
        wc_w = [sb("wc_w%d" % h, [P, KP], U32) for h in range(2)]
        wc_s = [sb("wc_s%d" % h, [P, KP], U8) for h in range(2)]
        wa_w = [[sb("wa_w%d%d" % (h, a), [P, KP], U32) for a in range(2)] for h in range(2)]
        wa_s = [[sb("wa_s%d%d" % (h, a), [P, KP], U8) for a in range(2)] for h in range(2)]
        minus_tanh = [[sb("minus_tanh%d%d" % (h, jb), [P, KP], F32) for jb in range(BLOCKS)] for h in range(2)]
        reading = [sb("reading%d" % jb, [P, KP], F32) for jb in range(BLOCKS)]
        h1 = [sb("h1_%d" % t, [P, S], F32) for t in range(PACK)]
        h2 = [sb("h2_%d" % t, [P, S], F32) for t in range(PACK)]
        x_w = [sb("x_w%d" % h, [P, PICK], U32) for h in range(2)]
        x_s = [sb("x_s%d" % h, [P, PICK], U8) for h in range(2)]

        def load_scales(dst, src, quadrants):
            for q in quadrants:
                nc.sync.dma_start(
                    out=dst[32 * q : 32 * q + 4, :].bitcast(I32).rearrange("p (a c) -> p a c", a=src.shape[0]),
                    in_=src[:, 4 * q : 4 * q + 4, :].bitcast(I32).rearrange("a r c -> r a c"),
                )

        def move_scales(a, quadrants):
            for q in quadrants:
                first = 16 * a + 4 * q
                nc.sync.dma_start(
                    out=v_s[a][32 * q : 32 * q + 4, :].bitcast(I32), in_=v_rows[first : first + 4, :].bitcast(I32)
                )

        def load_words(dst, src):
            nc.sync.dma_start(out=dst[:].bitcast(I32), in_=src.rearrange("p c i -> p (c i)").bitcast(I32))

        def load_wb(h):
            nc.sync.dma_start(
                out=wb_w[h].bitcast(I32).rearrange("p (a c) -> p a c", a=2),
                in_=wb_words[:, :, 2 * KP * h : 2 * KP * (h + 1)].bitcast(I32).rearrange("a p c -> p a c"),
            )

        def load_raw(dst, w, a, h):
            nc.sync.dma_start(
                out=dst[:].rearrange("p (i c) -> p i c", i=PACK),
                in_=w[KP * a : KP * (a + 1), KP * h : KP * (h + 1)].rearrange("(p i) c -> p i c", i=PACK),
            )

        def load_per_row(dst, vec, h):
            nc.sync.dma_start(out=dst[h][:], in_=vec[KP * h : KP * (h + 1)].rearrange("(p t) -> p t", t=PACK))

        def load_page(i):
            h, t = divmod(i, PACK)
            rows = page0[KP * h : KP * (h + 1), :].rearrange("(p t) c -> p t c", t=PACK)
            nc.sync.dma_start(out=pages[PAGE_BUFFER[i]][:], in_=rows[:, t, :])

        def gather(dst, window, offsets):
            nc.vector.tensor_copy(dst, window.indirect(offsets))

        def quantize(words, scales, woven, first, last):
            nc.vector.quantize_mx(
                out=words[:, first:last].bitcast(FP8X4), scales=scales[:, first:last],
                in_=woven[:, PACK * first : PACK * last],
            )

        def turn_gate(rows):
            for jb in range(BLOCKS):
                dst = banks[2 + jb // 2][:, P * (jb % 2) : P * (jb % 2 + 1)]
                nc.tensor.transpose(dst, rows[:, P * jb : P * (jb + 1)], ident[:])

        def deal_gate(dst, t):
            for u in range(2):
                rows = banks[2 + u][:, : 2 * P].rearrange("p (jb m t) -> p jb m t", jb=2, t=PACK)[:, :, :, t]
                nc.scalar.copy(
                    turned[t % 2][:, 2 * P * u : 2 * P * (u + 1)].rearrange("p (jb q m) -> p jb q m", jb=2, q=QUADS),
                    rows.unsqueeze(2).to_broadcast([P, 2, QUADS, 32]),
                )
            for jb in range(BLOCKS):
                cols = slice(P * jb, P * (jb + 1))
                nc.tensor.transpose(banks[t % 2][:, cols], turned[t % 2][:, cols], ident[:])
            nc.scalar.copy(dst[:], banks[t % 2][:])

        def round_wc(u, woven, src, copy):
            copy(
                woven[:, PICK * u : PICK * (u + 1)].rearrange("p (t m i) -> p m i t", t=2, i=PACK),
                src[:].rearrange("p (i m t) -> p m i t", i=PACK, t=PACK)[:, :, :, 2 * u : 2 * u + 2],
            )

        def round_wa(woven, src, copy):
            for u in range(2):
                part = slice(P // 2 * u, P // 2 * (u + 1))
                copy(
                    woven.rearrange("p (c e i) -> p c i e", e=4, i=PACK)[:, part],
                    src[:].rearrange("p (i c e) -> p c i e", i=PACK, e=4)[:, part],
                )

        def barcode(h, t):
            cols = slice(P * t, P * (t + 1))
            nc.tensor.matmul_mx(
                out=banks[4 + t][:], lhsT=wc_w[h][:, cols].bitcast(FP8X4), lhsT_scale=wc_s[h][:, cols],
                rhs=v2_w[:].bitcast(FP8X4), rhs_scale=v2_s[:], start=True, stop=True,
            )
            nc.scalar.activation(h2[t][:], banks[4 + t][:], ACT.Identity, bias=bias[h][:, t : t + 1])

        def line_product(bank, jb, a, rhs, rhs_scale):
            cols = slice(P * jb, P * (jb + 1))
            nc.tensor.matmul_mx(
                out=bank[:], lhsT=v_w[a][:, cols].bitcast(FP8X4), lhsT_scale=v_s[a][:, cols],
                rhs=rhs, rhs_scale=rhs_scale, start=(a == 0), stop=(a == 1),
            )

        def product_b(bank, h, jb, a):
            words = wb_w[h][:, 2 * KP * a : 2 * KP * (a + 1)].bitcast(FP4X4)
            line_product(bank, jb, a, words, wb_s[h][:, KP * a : KP * (a + 1)])

        def by_tile_in(bank):
            return bank[:].rearrange("p (m t) -> p t m", t=PACK)

        def by_tile_out(dst):
            return dst[:].rearrange("p (t m) -> p t m", t=PACK)

        def tanh_b(bank, h, jb):
            nc.scalar.activation(by_tile_out(minus_tanh[h][jb]), by_tile_in(bank), ACT.Tanh, scale=-1.0)

        def reading_a(h):
            for a in range(2):
                for jb in range(BLOCKS):
                    line_product(banks[4 + jb], jb, a, wa_w[h][a][:].bitcast(FP8X4), wa_s[h][a][:])
            for u in range(2):
                for jb in range(BLOCKS):
                    tiles = slice(2 * u, 2 * u + 2)
                    nc.scalar.copy(by_tile_out(reading[jb])[:, tiles, :], by_tile_in(banks[4 + jb])[:, tiles, :])

        def mismatch(h, t):
            cols = slice(P * t, P * (t + 1))
            for jb in range(BLOCKS):
                dst = banks[t % 2][:, P * jb : P * (jb + 1)]
                nc.tensor.matmul(dst, reading[jb][:, cols], ident[:], start=True, stop=False, is_transpose=True)
                nc.tensor.matmul(dst, minus_tanh[h][jb][:, cols], ident[:], start=False, stop=True, is_transpose=True)
            nc.scalar.activation(h1[t][:], banks[t % 2][:], ACT.Square)

        def put_barcode(i):
            window = pages[PAGE_BUFFER[i]][:].indirect(list4[:])
            nc.vector.tensor_tensor(window, h2[i % PACK][:], gate2[i % PACK][:], MULT)

        def put_line(i):
            window = pages[PAGE_BUFFER[i]][:].indirect(list3[:])
            nc.vector.tensor_tensor(window, h1[i % PACK][:], gate1[i % PACK][:], MULT)

        def fetch(i, dst):
            gather(dst, pages[PAGE_BUFFER[i]][:], list5[:])

        def log_abs(pieces):
            for piece in pieces:
                nc.scalar.activation(piece, piece, ACT.Abs)
            for piece in pieces:
                nc.scalar.activation(piece, piece, ACT.Ln, bias=1.0)

        def compress(i, picked, x_rows):
            h, t = divmod(i, PACK)
            log_abs([picked[:, S * u : S * (u + 1)] for u in range(2)])
            for u in range(2):
                dst = x_rows[:, PICK * t + S * u : PICK * t + S * (u + 1)]
                nc.scalar.activation(dst, picked[:, S * u : S * (u + 1)], ACT.Copy, scale=gains[h][:, t : t + 1])

        def weave(woven, x_rows, tiles):
            for u in range(2):
                part = slice(P * u, P * (u + 1))
                nc.scalar.copy(
                    woven[:].rearrange("p (c e t) -> p c t e", e=4, t=PACK)[:, part, :tiles, :],
                    x_rows[:].rearrange("p (t c e) -> p c t e", t=PACK, e=4)[:, part, :tiles, :],
                )

        def score(s, h):
            cols = slice(SLICE * s, SLICE * (s + 1))
            for n in range(N // P):
                wo_cols = slice(N * h + P * n, N * h + P * (n + 1))
                nc.tensor.matmul_mx(
                    out=banks[2 * s + n // 2][:, SLICE * (n % 2) : SLICE * (n % 2 + 1)],
                    lhsT=wo_w[:, wo_cols].bitcast(FP8X4), lhsT_scale=wo_s[:, wo_cols],
                    rhs=x_w[h][:, cols].bitcast(FP8X4), rhs_scale=x_s[h][:, cols],
                    start=(h == 0 and n % 2 == 0), stop=(h == 1 and n % 2 == 1),
                )

        def store(s, first, banks_stored):
            nc.sync.dma_start(
                out=out[2 * P * first : 2 * P * (first + banks_stored), SLICE * s : SLICE * (s + 1)].rearrange(
                    "(n p) c -> p n c", p=P
                ),
                in_=raw[s][:, BANK * first : BANK * (first + banks_stored)].rearrange("p (n c) -> p n c", c=SLICE),
            )

        for unused in (slice(32, 64), slice(64, P)):
            nc.vector.memset(tab_s[unused, :].bitcast(I32), 0)
        for scales in (tab2_s, wb_s[0], v_s[0], v_s[1], wb_s[1], wo_s):
            nc.vector.memset(scales[:].bitcast(I32), 0)
        make_identity(nc, ident[:])

        nc.sync.dma_start(out=wg2_rows[:], in_=wg2)
        nc.sync.dma_start(list1[:], offs)
        nc.sync.dma_start(out=tab_s[0:32, :].bitcast(I32), in_=tab_scales.rearrange("a r c -> (a r) c").bitcast(I32))
        nc.sync.dma_start(list2[:], offs2)
        load_words(tab2_w, tab2_words[0])
        load_raw(raw[0], wc, 0, 0)
        nc.sync.dma_start(list4[:], offs4)
        load_per_row(bias, bc, 0)
        load_scales(tab2_s, tab2_scales, (0, 2, 1, 3))
        load_page(0)
        nc.sync.dma_start(out=wg1_rows[:], in_=wg1)
        gather(v_rows[:], tab_s[:], list1[:])
        move_scales(0, (0, 1, 2))
        load_words(tab_w[0], tab_words[0])
        move_scales(0, (3,))
        move_scales(1, (0, 1))
        load_page(1)
        move_scales(1, (2, 3))
        load_scales(wb_s[0], wb_scales[:, :, :KP], (0, 2))
        load_words(tab_w[1], tab_words[1])
        load_scales(wb_s[0], wb_scales[:, :, :KP], (1, 3))
        load_wb(0)
        load_raw(raw[1], wa, 0, 0)
        load_raw(raw[2], wa, 1, 0)
        load_page(2)
        load_page(3)
        nc.sync.dma_start(list3[:], offs3)
        load_wb(1)
        load_scales(wb_s[1], wb_scales[:, :, KP:], (0, 2, 1, 3))
        nc.sync.dma_start(list5[:], offs5)
        load_per_row(gains, gain, 0)
        load_raw(raw[3], wc, 0, 1)

        gather(v2_w[:], tab2_w[:], list2[:])
        turn_gate(wg2_rows)
        for t in range(2):
            deal_gate(gate2[t], t)
        round_wc(0, stage[0], raw[0], nc.vector.tensor_copy)
        gather(v2_s[:], tab2_s[:], list2[:])
        quantize(wc_w[0], wc_s[0], stage[0], 0, KP // 2)
        round_wc(1, stage[0], raw[0], nc.scalar.copy)
        for t in range(2):
            barcode(0, t)
        put_barcode(0)
        quantize(wc_w[0], wc_s[0], stage[0], KP // 2, KP)
        load_raw(raw[0], wa, 0, 1)
        for t in range(2, PACK):
            deal_gate(gate2[t], t)
            barcode(0, t)
        turn_gate(wg1_rows)
        gather(v_w[0][:], tab_w[0][:], list1[:])
        put_barcode(1)
        gather(v_w[1][:], tab_w[1][:], list1[:])
        for t in range(PACK):
            deal_gate(gate1[t], t)
        for a in range(2):
            for jb in range(BLOCKS):
                product_b(banks[jb], 0, jb, a)
        for a in range(2):
            round_wa(stage[1 - a][:], raw[1 + a], nc.vector.tensor_copy)
            for first in (0, KP // 2):
                quantize(wa_w[0][a], wa_s[0][a], stage[1 - a], first, first + KP // 2)
        for jb in range(BLOCKS):
            tanh_b(banks[jb], 0, jb)
        load_raw(raw[1], wa, 1, 1)
        load_per_row(bias, bc, 1)
        load_per_row(gains, gain, 1)
        load_scales(wo_s, wo_scales, range(QUADS))
        nc.sync.dma_start(
            out=wo_w[:].bitcast(I32).rearrange("p (a c) -> p a c", a=2),
            in_=wo_words.rearrange("a p c i -> p a (c i)").bitcast(I32),
        )
        load_page(6)
        reading_a(0)
        for t in range(2, PACK):
            put_barcode(t)
        for t in range(PACK):
            mismatch(0, t)
            put_line(t)

        for jb in range(BLOCKS):
            for a in range(2):
                product_b(banks[jb % 2], 1, jb, a)
            tanh_b(banks[jb % 2], 1, jb)

        middle = sb("middle", [P, 6 * PICK], F32, over="wb_w1")
        overlap = PICK // 4

        def span(first):
            return middle[:, first : first + PICK]

        woven_wc = span(0).bitcast(BF16)
        woven_wa = [span(2 * PICK - overlap).bitcast(BF16), span(4 * PICK + overlap).bitcast(BF16)]
        picked = [span(PICK - overlap), span(3 * PICK - 2 * overlap), span(4 * PICK - 2 * overlap), span(5 * PICK)]
        picked.extend(raw[t][:, PICK:] for t in range(PACK - 1))

        for u in range(2):
            round_wc(u, woven_wc, raw[3], nc.scalar.copy)
        quantize(wc_w[1], wc_s[1], woven_wc, 0, KP)
        fetch(0, picked[0])
        round_wa(woven_wa[0], raw[0], nc.scalar.copy)
        quantize(wa_w[1][0], wa_s[1][0], woven_wa[0], 0, KP)
        fetch(1, picked[1])
        load_page(4)
        round_wa(woven_wa[1], raw[1], nc.scalar.copy)
        quantize(wa_w[1][1], wa_s[1][1], woven_wa[1], 0, KP)
        fetch(2, picked[2])
        load_page(5)
        fetch(3, picked[3])

        for t in range(PACK):
            barcode(1, t)
        x_rows = sb("x_rows", [P, PACK * PICK], BF16, over="page0")
        for i in range(2):
            compress(i, picked[i], x_rows)
        reading_a(1)
        for t in range(PACK):
            mismatch(1, t)
        woven_x = [sb("woven_x%d" % h, [P, PICK * PACK], BF16, over="tab_w%d" % h) for h in range(2)]
        for i in range(2, PACK):
            compress(i, picked[i], x_rows)
        weave(woven_x[0], x_rows, PACK)

        for i in range(PACK, LAST):
            put_barcode(i)
        put_line(4)
        put_line(5)
        fetch(4, picked[4])
        compress(4, picked[4], x_rows)
        load_page(LAST)
        fetch(5, picked[5])
        compress(5, picked[5], x_rows)
        put_line(6)
        fetch(6, picked[6])
        compress(6, picked[6], x_rows)
        weave(woven_x[1], x_rows, PACK - 1)

        for first, last in ((0, SLICE), (SLICE, 3 * SLICE), (3 * SLICE, PICK)):
            quantize(x_w[0], x_s[0], woven_x[0], first, last)
        put_barcode(LAST)
        put_line(LAST)
        for s in range(SLICES):
            score(s, 0)

        tail = woven_x[0][:, PACK * SLICE : PACK * 3 * SLICE].bitcast(F32)
        pieces = [tail[:, SLICE * s : SLICE * (s + 1)] for s in range(SLICES)]
        last_place = woven_x[1][:].rearrange("p (j t) -> p j t", t=PACK)[:, :, PACK - 1]
        for s in range(SLICES):
            offsets = list5[:, SLICE // 16 * s : SLICE // 16 * (s + 1)]
            gather(pieces[s], pages[PAGE_BUFFER[LAST]][:], offsets)
        for s0 in range(0, SLICES, 2):
            log_abs(pieces[s0 : s0 + 2])
            for s in (s0, s0 + 1):
                dst = last_place[:, SLICE * s : SLICE * (s + 1)]
                nc.vector.tensor_scalar(dst, pieces[s], gains[1][:, PACK - 1 : PACK], None, MULT)
            for s in (s0, s0 + 1):
                quantize(x_w[1], x_s[1], woven_x[1], SLICE * s, SLICE * (s + 1))
                score(s, 1)

        for s in range(SLICES - 1):
            for u in range(2):
                nc.scalar.copy(raw[s][:, BANK * u : BANK * (u + 1)], banks[2 * s + u][:])
                store(s, u, 1)
        nc.vector.tensor_copy(raw[SLICES - 1][:, :BANK], banks[2 * SLICES - 2][:])
        nc.scalar.copy(raw[SLICES - 1][:, BANK : 2 * BANK], banks[2 * SLICES - 1][:])
        store(SLICES - 1, 0, 2)
